import numpy as np, ml_dtypes
CORES = [40,64,80,88,96,104,120,144]
N = 8
BF = ml_dtypes.bfloat16
def gentries(a):
    return np.ascontiguousarray(a.reshape(8, 16, -1).transpose(0, 2, 1)).reshape(8, -1)
def gtable(e):
    e = np.asarray(e); return np.ascontiguousarray(e.reshape(8, -1, 16).transpose(0, 2, 1)).reshape(128, -1).astype(np.int32)
P, S, H, C, D, TH = 1024, 160, 2048, 4, 3, 11008
W = P + (N - 1) * S
def stored(v):
    return np.stack([gtable(np.reshape(v[r], (8, -1))) for r in range(N)])
def setup_inputs(rng):
    v = rng.integers(0, 8, (N, 8, 16, P)) + rng.integers(32, 128, (N, 8, 1, P)) * (np.arange(16)[:, None] == rng.integers(0, 16, (N, 8, 1, P)))
    return {"x": v.reshape(N, 128, P).astype(np.float32).astype(BF), "sus": np.floor(256 * rng.random((N, 128, H)) ** 2).astype(np.float32).astype(BF),
            "hist": stored(rng.integers(0, H, (N, 8, P))), "home": stored(rng.integers(0, W, (N, 8, C, P))), "away": stored(rng.integers(0, W, (N, 8, C, P))),
            "shown": stored(rng.integers(0, P, (N, 8, N - 1, S)))}
def setup_inputs_ties(rng):
    d = setup_inputs(rng); b = TH // 64
    d["x"] = (64 * (rng.random((N, 128, P)) * C < 0.25)).astype(np.float32).astype(BF)
    d["sus"] = rng.choice(np.array([0, 0, b, b + 1]), (N, 128, H)).astype(np.float32).astype(BF); return d
def setup_inputs_ends(rng):
    d = setup_inputs(rng); e = np.array([0, P - 1] + [P + k * S for k in range(N - 1)] + [P + k * S + S - 1 for k in range(N - 1)])
    for a, w in (("home", e), ("away", e), ("shown", e[:2]), ("hist", np.array([0, 15, H - 16, H - 1]))):
        d[a] = np.where(rng.random(d[a].shape) < 0.5, rng.choice(w, d[a].shape), d[a]).astype(np.int32)
    return d
def setup_inputs_one(rng):
    d = setup_inputs(rng); o = np.ones((1, 1, P), np.int64)
    d["hist"] = stored(rng.integers(0, H, (N, 8, 1)) * o); d["home"] = stored(rng.integers(0, W, (N, 8, 1)) * np.ones((1, 1, C * P), np.int64)); return d
def setup_inputs_far(rng):
    d = setup_inputs(rng); own = rng.integers(0, P, (N, 8, C, P)); out = rng.integers(P, W, (N, 8, C, P)); even = (np.arange(N) % 2 == 0)[:, None, None, None]
    d["home"] = stored(np.where(even, out, own)); d["away"] = stored(np.where(even, own, out)); return d
def setup_inputs_spread(rng):
    d = setup_inputs(rng); s = np.where(rng.random((N, 8, 1, P)) < 0.5, rng.integers(0, 4, (N, 8, 1, P)), rng.integers(0, 9, (N, 8, 1, P)))
    d["x"] = np.floor(256 * rng.random((N, 8, 16, P)) * np.exp2(-s)).reshape(N, 128, P).astype(np.float32).astype(BF)
    d["sus"] = np.floor(256 * rng.random((N, 8, 16, H)) * np.exp2(-rng.integers(0, 6, (N, 8, 1, H)))).reshape(N, 128, H).astype(np.float32).astype(BF)
    for a, n, k in (("hist", H, P), ("home", W, C * P), ("away", W, C * P), ("shown", P, (N - 1) * S)):
        d[a] = stored((np.floor(n * rng.random((N, 8, k)) ** 3).astype(np.int64) + rng.integers(0, n, (N, 8, 1))) % n)
    return d
def check_inputs(d):
    bad = []
    for a in ("x", "sus"):
        v = d[a].astype(np.float32)
        if not ((v >= 0) & (v <= 255) & (v == np.floor(v))).all(): bad.append(a)
    for a, n in (("hist", H), ("home", W), ("away", W), ("shown", P)):
        if not ((d[a] >= 0) & (d[a] < n)).all(): bad.append(a)
    return bad
def reference(x, sus, hist, home, away, shown):
    load = x.astype(np.float32).astype(np.int64).reshape(N, 8, 16, P); tab = sus.astype(np.float32).astype(np.int64).reshape(N, 8, 16, H)
    code = np.stack([gentries(hist[r]) for r in range(N)]).astype(np.int64); ill = np.zeros((N, 8, P), bool)
    near = np.stack([gentries(home[r]) for r in range(N)]).reshape(N, 8, C, P); far = np.stack([gentries(away[r]) for r in range(N)]).reshape(N, 8, C, P)
    give = np.stack([gentries(shown[r]) for r in range(N)]).reshape(N, 8, N - 1, S)
    for day in range(D):
        new = load >> 1
        for r in range(N):
            parts = [load[r]]
            for q in range(N):
                if q != r: parts.append(np.take_along_axis(load[q], give[q][:, None, r if r < q else r - 1], 2))
            win = np.concatenate(parts, 2)
            con = np.where(ill[r][:, None], far[r], near[r]).reshape(8, 1, C * P)
            pressure = np.sum(np.take_along_axis(win, con, 2).reshape(8, 16, C, P), axis=2)
            score = pressure * np.take_along_axis(tab[r], code[r][:, None], 2)
            best = np.argmax(score, axis=1); hit = np.max(score, axis=1) > TH
            new[r] += 64 * ((np.arange(16)[:, None] == best[:, None]) & hit[:, None])
            code[r] = np.where(hit, (16 * code[r] + best) & (H - 1), code[r]); ill[r] = hit
        load = new
    return {"y": load.reshape(N, 128, P).astype(np.float32), "h": stored(code).astype(np.float32)}

@@ -1,0 +1,459 @@
+from concourse.bass import DstId, RemoteDMATransfer
+from concourse.mybir import AluOpType, ActivationFunctionType
+
+P, S, D, TH = 1024, 160, 3, 11008
+W = P + 7 * S
+NSEM = 60
+BF, F32, I32, U16 = "bfloat16", "float32", "int32", "uint16"
+SCRATCH = {}
+for _d in range(D):
+    SCRATCH["win%d" % _d] = ("sbuf", [128, W], BF)
+    SCRATCH["snd%d" % _d] = ("sbuf", [128, 7 * S], BF)
+for _n, _c, _t in (
+        ("ybuf", P, F32), ("susb", 2048, BF), ("shi", 70, I32), ("shu", 70, U16), ("homi", 256, I32), ("awyi", 256, I32),
+        ("homf", 256, F32), ("awyf", 256, F32), ("dif", 256, F32), ("tmpo", 256, F32), ("offf", 256, F32), ("offu", 256, U16),
+        ("hsi", 64, I32), ("cf", 64, F32), ("cu", 64, U16), ("ci", 64, I32), ("c7", 64, I32), ("ct", 64, F32), ("af", 64, F32),
+        ("hit", 64, F32), ("uu", 64, F32), ("tt", 64, F32), ("hout", 64, F32),
+        ("gth", 4096, BF), ("sg", P, BF), ("st", P, BF), ("sc", P, F32), ("kk", P, F32), ("ki", 64, I32), ("ri", 64, I32),
+        ("ee", 128, BF), ("et", 128, BF), ("rr", 512, BF), ("hy", P, BF), ("half", P, BF),
+        ("ident", 128, BF), ("d0", 512, BF), ("wz0", 256, BF), ("wz", 1024, BF), ("m4", 4, F32), ("dg", 128, BF),
+        ("ones", 512, BF), ("mk", 8, F32),
+        ("wd", 240, BF), ("pci", 8, I32), ("pcf", 8, F32), ("pd", 8, F32), ("cc", 240, F32), ("pmf", 36, F32), ("pmu", 36, U16),
+        ("ia", 256, F32), ("ib", 256, F32), ("wa", 256, F32), ("wb", 256, F32)):
+    SCRATCH[_n] = ("sbuf", [128, _c], _t)
+for _n in ("p0", "p1", "p2", "z0", "z1", "z2", "fx"):
+    SCRATCH[_n] = ("psum", [128, 512], F32)
+SEMAPHORES = ["sent", "arr0", "arr1", "arr2", "rin0", "rin1", "rin2"] + ["s%d" % _i for _i in range(NSEM)]
+
+A = AluOpType
+ACT = ActivationFunctionType
+EARLY_MASKS = 5
+
+
+def routes(T, topo):
+    cores = list(T.cores)
+    out = []
+    for r, c in enumerate(cores):
+        near = [q for q, x in enumerate(cores) if q != r and topo.may_write(c, x)]
+        far = [q for q, x in enumerate(cores) if q != r and not topo.may_write(c, x)]
+        hs = [x for x in topo.cores_of(c) if x not in cores and all(topo.may_write(x, cores[q]) for q in far)]
+        same = [x for x in hs if topo.die(x) == topo.die(c)]
+        other = [x for x in hs if topo.die(x) != topo.die(c)]
+        hs = [x for pair in zip(same, other) for x in pair]
+        ring = sorted(near + [r])
+        i = ring.index(r)
+        n = len(hs)
+        by_helper = [None] * n
+        for j, q in enumerate(far):
+            by_helper[(i + j) % n] = q
+        near = [ring[(i + t) % len(ring)] for t in range(1, len(ring))]
+        out.append(([(by_helper[t], hs[t]) for t in range(n)], near))
+    return out
+
+
+def bits(es):
+    m = 0
+    for e in es:
+        m |= 1 << e
+    return m
+
+
+def near_masks(c, cores, near, topo):
+    e = topo.engines(c, cores[near[0]])
+    h = len(e) // 2
+    return [e[:h], e[h:], e]
+
+
+def slot(r, q):
+    return P + S * (r if r < q else r - 1)
+
+
+def add(pl, q, fn, reads=(), writes=(), dma=False, acc=False, ext=None):
+    i = len(pl["ops"])
+    deps = set()
+    for k in reads:
+        st = pl["keys"].setdefault(k, [[], []])
+        deps.update(st[0])
+    for k in writes:
+        st = pl["keys"].setdefault(k, [[], []])
+        deps.update(st[1])
+        deps.update(w for w in st[0] if not (acc and pl["ops"][w]["q"] == q))
+    for k in reads:
+        pl["keys"][k][1].append(i)
+    for k in writes:
+        st = pl["keys"][k]
+        if acc and not st[1]:
+            st[0].append(i)
+        else:
+            pl["keys"][k] = [[i], []]
+    deps.discard(i)
+    pl["ops"].append({"q": q, "fn": fn, "deps": deps, "dma": dma, "ext": ext})
+
+
+def emit(pl, queues, T):
+    ops = pl["ops"]
+    know = {q: set() for q in queues}
+    for i, o in enumerate(ops):
+        if o["ext"]:
+            o["know"], o["waits"], o["before"] = {i}, [], set()
+            continue
+        kn = know[o["q"]]
+        o["waits"] = []
+        for j in sorted(o["deps"], reverse=True):
+            if j not in kn:
+                o["waits"].append(j)
+                kn |= ops[j]["know"]
+                ops[j]["need"] = True
+        o["before"] = set(kn)
+        o["know"] = set(kn) | {i}
+    sems = []
+    for i, o in enumerate(ops):
+        if o["ext"]:
+            o["tok"] = o["ext"]
+            continue
+        eng = queues[o["q"]]
+        for j in o["waits"]:
+            eng.wait_ge(T.sem[ops[j]["tok"][0]], ops[j]["tok"][1])
+        if o["fn"] is None:
+            continue
+        ins = o["fn"]()
+        if o.get("need"):
+            n = 16 if o["dma"] else 1
+            pick = None
+            for s in sems:
+                if s[2] == o["dma"] and s[1] in o["before"]:
+                    pick = s
+                    break
+            if pick is None:
+                pick = ["s%d" % len(sems), i, o["dma"], 0]
+                sems.append(pick)
+            pick[1] = i
+            pick[3] += n
+            o["tok"] = (pick[0], pick[3])
+            ins.then_inc(T.sem[pick[0]], n)
+
+
+def helper_program(g, core, T, topo, r, q):
+    cores = list(T.cores)
+    rid, pid = topo.addr(cores[q], core)
+    n_in = len(topo.engines(cores[r], core)) // 4
+    e = topo.engines(core, cores[q])
+    for d in range(D):
+        g.wait_ge(T.sem["rin%d" % d], n_in)
+        c0 = slot(r, q)
+        g.remote_dma(T["win%d" % d][:, c0:c0 + S], T["snd%d" % d][:, 0:S], T.sem["arr%d" % d], T.sem.sent, pid, rid, bits(e))
+    g.wait_ge(T.sem.sent, D * len(e))
+
+
+def rank_program(g, core, T, topo):
+    rt = routes(T, topo)
+    cores = list(T.cores)
+    rank = T.rank_of(core)
+    if rank is None:
+        for r in range(len(cores)):
+            for q, h in rt[r][0]:
+                if h == core:
+                    helper_program(g, core, T, topo, r, q)
+        return
+    far, near = rt[rank]
+    n_arr = 0
+    for r in range(len(cores)):
+        for q, h in rt[r][0]:
+            if q == rank:
+                n_arr += len(topo.engines(h, core))
+        if rank in rt[r][1]:
+            n_arr += len(near_masks(cores[r], cores, rt[r][1], topo)[rt[r][1].index(rank)])
+    order = [q for q, h in far] + near
+    V, AC, PE, SY = g.vector, g.scalar, g.tensor, g.sync
+    queues = {"v": V, "a": AC, "p": PE, "s": SY, "g": g}
+    pl = {"ops": [], "keys": {}}
+    sent = [0]
+
+    def v(fn, r, w):
+        add(pl, "v", fn, r, w)
+
+    def a(fn, r, w):
+        add(pl, "a", fn, r, w)
+
+    def pe(mms, r, w):
+        def fn():
+            ins = None
+            for m in mms:
+                ins = PE.matmul(*m)
+            return ins
+        add(pl, "p", fn, r, w, acc=True)
+
+    def load(qn, out, in_, r, w):
+        add(pl, qn, lambda: queues[qn].dma_start(out, in_), r, w, dma=True)
+
+    def ts(out, in0, s1, s2, op0, op1, r, w):
+        if op1 is None:
+            v(lambda: V.tensor_scalar(out, in0, s1, None, op0), r, w)
+        else:
+            v(lambda: V.tensor_scalar(out, in0, s1, s2, op0, op1), r, w)
+
+    def tt(out, in0, in1, op, r, w):
+        v(lambda: V.tensor_tensor(out, in0, in1, op), r, w)
+
+    def cp(out, in_, r, w):
+        v(lambda: V.tensor_copy(out, in_), r, w)
+
+    def acp(out, in_, r, w, scale=1.0):
+        a(lambda: AC.activation(out, in_, ACT.Copy, scale=scale), r, w)
+
+    def iota(out, pat, base, cm, w, flt=True):
+        if flt:
+            add(pl, "g", lambda: g.iota(out, pat, base, cm, allow_small_or_imprecise_dtypes=True), [], w)
+        else:
+            add(pl, "g", lambda: g.iota(out, pat, base, cm), [], w)
+
+    def own(d):
+        return ["oA%d" % d, "oB%d" % d, "oC%d" % d]
+
+    def conv_shown(t0, t1):
+        for t in range(t0, t1):
+            q = order[t]
+            k = q if q < rank else q - 1
+            cp(T.shu[:, 10 * t:10 * t + 10], T.shi[:, 10 * k:10 * k + 10], ["shi"], ["shu%d" % t])
+
+    def gather_shown(d, eng, t0, t1):
+        src = T["win%d" % d][:, 0:P].indirect(T.shu[:, 10 * t0:10 * t1])
+        (acp if eng == "a" else cp)(T["snd%d" % d][:, S * t0:S * t1], src, own(d) + ["shu%d" % t for t in range(t0, t1)],
+                                    ["snd%d_%d" % (d, t) for t in range(t0, t1)])
+
+    def send_far(d):
+        def fn():
+            trs = []
+            for t, (q, h) in enumerate(far):
+                rid, pid = topo.addr(h, core)
+                e = topo.engines(core, h)[t::len(far)]
+                trs.append(RemoteDMATransfer(dst_ids=[DstId(rid=rid, pnc=pid)], dma_engine_mask=bits(e),
+                                             remote_sem=T.sem["rin%d" % d], src=T["snd%d" % d][:, S * t:S * t + S],
+                                             dst=T["snd%d" % d][:, 0:S]))
+                sent[0] += len(e)
+            return g.remote_dma_fused(trs, local_sem=T.sem.sent)
+        add(pl, "g", fn, ["snd%d_%d" % (d, t) for t in range(4)], [])
+
+    def send_near(d, js):
+        def fn():
+            trs = []
+            for j in js:
+                q = near[j]
+                rid, pid = topo.addr(cores[q], core)
+                e = near_masks(core, cores, near, topo)[j]
+                c0 = slot(rank, q)
+                trs.append(RemoteDMATransfer(dst_ids=[DstId(rid=rid, pnc=pid)], dma_engine_mask=bits(e),
+                                             remote_sem=T.sem["arr%d" % d], src=T["snd%d" % d][:, S * (4 + j):S * (5 + j)],
+                                             dst=T["win%d" % d][:, c0:c0 + S]))
+                sent[0] += len(e)
+            return g.remote_dma_fused(trs, local_sem=T.sem.sent)
+        add(pl, "g", fn, ["snd%d_%d" % (d, 4 + j) for j in js], [])
+
+    def col(t, j):
+        return t[:, j:j + 1]
+
+    def masks(u0, u1):
+        for u in range(u0, u1):
+            a(lambda u=u: AC.activation(T.rr[:, 64 * u:64 * u + 64], T.ee[:, 0:128:2], ACT.Identity, scale=col(T.mk, u)),
+              ["eA", "eB", "mk"], ["rr%d" % u])
+
+    def fix():
+        pe([(T.fx[:, 0:64], T.wd[:, 112 - 16 * k:240 - 16 * k], T.rr[:, k:512:8], k == 0, k == 7) for k in range(8)],
+           ["wd"] + ["rr%d" % u for u in range(8)], ["fx"])
+
+    def history():
+        ts(T.hit[:], T.fx[:, 0:64], 16.0, None, A.is_lt, None, ["fx"], ["hit"])
+        tt(T.uu[:], T.af[:], T.fx[:, 0:64], A.subtract, ["af", "fx"], ["uu"])
+        tt(T.tt[:], T.uu[:], T.hit[:], A.mult, ["uu", "hit"], ["tt"])
+        tt(T.cf[:], T.tt[:], T.cf[:], A.add, ["tt", "cf"], ["cf"])
+
+    def suscept():
+        for k in range(2):
+            acp(T.sg[:, 512 * k:512 * k + 512], T.susb[:, 0:2048].indirect(T.cu[:, 32 * k:32 * k + 32]), ["susb", "cu"],
+                ["sg%d" % k], scale=32.0)
+        for k in range(2):
+            pb = T["p%d" % k]
+            for b in range(4):
+                pe([(pb[:, 128 * b:128 * b + 128], T.sg[:, 512 * k + 128 * b:512 * k + 128 * b + 128], T.ident[:], True, True)],
+                   ["sg%d" % k, "ident"], ["p%d" % k])
+        for k in range(2):
+            acp(T.st[:, 512 * k:512 * k + 512], T["p%d" % k][:], ["p%d" % k], ["st%d" % k])
+
+    def halves(d):
+        ts(T.hy[:], T["win%d" % d][:, 0:P], 0.5, 127.8, A.mult, A.add, own(d), ["hy"])
+        ts(T.half[:], T.hy[:], 128.0, None, A.subtract, None, ["hy"], ["half"])
+        for zn, c0, n in (("z0", 0, 512), ("z1", 512, 256), ("z2", 768, 256)):
+            pe([(T[zn][:, 0:n], T.ident[:], T.half[:, c0:c0 + n], True, False),
+                (T[zn][:, 0:n], T.dg[:], T.ones[:, 0:n], False, False)], ["ident", "half", "dg", "ones"], [zn])
+
+    def next_code():
+        cp(T.ci[:], T.cf[:], ["cf"], ["ci"])
+        ts(T.c7[:], T.ci[:], 127, None, A.bitwise_and, None, ["ci"], ["c7"])
+        ts(T.ct[:], T.c7[:], 16.0, 15.0, A.mult, A.add, ["c7"], ["ct"])
+        tt(T.af[:], T.ct[:], T.cf[:], A.subtract, ["ct", "cf"], ["af"])
+
+    load("s", T.win0[:, 0:P], T.x[:], [], own(0))
+    load("a", T.shi[:], T.shown[:], [], ["shi"])
+    load("s", T.susb[:], T.sus[:], [], ["susb"])
+    load("s", T.hsi[:], T.hist[:], [], ["hsi"])
+    load("s", T.homi[:], T.home[:], [], ["homi"])
+    load("s", T.awyi[:], T.away[:], [], ["awyi"])
+    iota(col(T.pci, 6), [[0, 1]], 0, 1, ["pi"], flt=False)
+    iota(T.pmf[:, 0:16], [[8, 8], [128, 2]], 0, 0, ["pmf0"])
+    iota(T.pmf[:, 16:32], [[1, 8], [0, 2]], 0, 0, ["pmf1"])
+    iota(T.pmf[:, 32:36], [[2, 4]], 0, 0, ["pmf2"])
+    iota(T.cc[:], [[1, 240]], 0, 0, ["cc"])
+    v(lambda: V.memset(T.d0[:], 1.0), [], ["d0"])
+    v(lambda: V.memset(T.ones[:], 1.0), [], ["ones"])
+    v(lambda: V.memset(T.d0[:, 0:512:16], -3.0e7), [], ["d0"])
+    pi = col(T.pci, 6)
+    ts(col(T.pci, 0), pi, 7, None, A.bitwise_and, None, ["pi"], ["pc0"])
+    ts(col(T.pci, 1), pi, 3, 1, A.arith_shift_right, A.bitwise_and, ["pi"], ["pc1"])
+    ts(col(T.pci, 2), pi, 15, None, A.bitwise_and, None, ["pi"], ["pc2"])
+    ts(col(T.pci, 3), pi, 4, None, A.arith_shift_right, None, ["pi"], ["pc3"])
+    ts(col(T.pci, 4), pi, 1, None, A.bitwise_and, None, ["pi"], ["pc4"])
+    ts(col(T.pci, 5), pi, 31, 1, A.bitwise_and, A.arith_shift_right, ["pi"], ["pc5"])
+    ts(col(T.pci, 7), pi, 5, None, A.arith_shift_right, None, ["pi"], ["pc6"])
+    conv_shown(0, 4)
+    gather_shown(0, "a", 0, 2)
+    gather_shown(0, "v", 2, 4)
+    send_far(0)
+    conv_shown(4, 7)
+    gather_shown(0, "a", 4, 6)
+    gather_shown(0, "v", 6, 7)
+    send_near(0, [0, 1])
+    send_near(0, [2])
+    iota(T.ia[:], [[1, 16], [0, 16]], 0, 0, ["ia"])
+    iota(T.ib[:], [[0, 16], [-1, 16]], 15, 0, ["ib"])
+    cp(T.cu[:], T.hsi[:], ["hsi"], ["cu"])
+    cp(T.pcf[:], T.pci[:], ["pi"] + ["pc%d" % j for j in range(7)], ["pcf"])
+    a7, hh, q16, uc, kd, q32, pf, quad = [col(T.pcf, j) for j in range(8)]
+    ts(T.ident[:], T.cc[:, 0:128], pf, None, A.is_equal, None, ["cc", "pcf"], ["ident"])
+    ts(col(T.pd, 0), a7, 8.0, hh, A.mult, A.add, ["pcf"], ["pd0"])
+    ts(col(T.pd, 1), a7, 8.0, None, A.mult, None, ["pcf"], ["pd1"])
+    ts(col(T.pd, 2), hh, 64.0, a7, A.mult, A.add, ["pcf"], ["pd2"])
+    ts(col(T.pd, 3), kd, -128.0, 128.0, A.mult, A.add, ["pcf"], ["pd3"])
+    ts(col(T.pd, 4), kd, -64.0, None, A.mult, None, ["pcf"], ["pd4"])
+    ts(col(T.pd, 5), q16, 15.0, None, A.subtract, None, ["pcf"], ["pd5"])
+    ts(T.pmu[:, 0:16], T.pmf[:, 0:16], col(T.pd, 2), None, A.add, None, ["pmf0", "pd2"], ["pmH"])
+    ts(T.pmu[:, 16:32], T.pmf[:, 16:32], col(T.pd, 1), None, A.add, None, ["pmf1", "pd1"], ["pmI"])
+    ts(T.pmu[:, 32:36], T.pmf[:, 32:36], col(T.pd, 0), None, A.add, None, ["pmf2", "pd0"], ["pm64"])
+    ts(col(T.pd, 6), col(T.pd, 5), col(T.pd, 5), -64.0, A.mult, A.mult, ["pd5"], ["pd6"])
+    cp(T.offu[:], T.homi[:].indirect(T.pmu[:, 0:16]), ["homi", "pmH"], ["offu"])
+    ts(col(T.pd, 7), col(T.pd, 6), 64.0, None, A.add, None, ["pd6"], ["pd7"])
+    suscept()
+    ts(T.dg[:], T.ident[:], col(T.pd, 7), None, A.mult, None, ["ident", "pd7"], ["dg"])
+    halves(0)
+    ts(T.wa[:], T.ia[:], q32, None, A.is_equal, None, ["ia", "pcf"], ["wa"])
+    ts(T.wb[:], T.ib[:], col(T.pd, 3), col(T.pd, 4), A.mult, A.add, ["ib", "pd3", "pd4"], ["wb"])
+    ts(T.mk[:], T.cc[:, 0:8], uc, None, A.is_equal, None, ["cc", "pcf"], ["mk"])
+    ts(T.m4[:], T.cc[:, 0:4], quad, None, A.is_equal, None, ["cc", "pcf"], ["m4"])
+    tt(T.wz0[:], T.wa[:], T.wb[:], A.mult, ["wa", "wb"], ["wz0"])
+    ts(T.wd[:], T.cc[:], 112.0, q16, A.subtract, A.is_equal, ["cc", "pcf"], ["wd"])
+    for k in range(4):
+        ts(T.wz[:, 256 * k:256 * k + 256], T.wz0[:], col(T.m4, k), None, A.mult, None, ["wz0", "m4"], ["wq%d" % k])
+    cp(T.cf[:], T.hsi[:].indirect(T.pmu[:, 32:36]), ["hsi", "pm64"], ["cf"])
+    cp(T.homf[:], T.homi[:].indirect(T.pmu[:, 0:16]), ["homi", "pmH"], ["homf"])
+    next_code()
+    cp(T.awyf[:], T.awyi[:].indirect(T.pmu[:, 0:16]), ["awyi", "pmH"], ["awyf"])
+    tt(T.dif[:], T.awyf[:], T.homf[:], A.subtract, ["awyf", "homf"], ["dif"])
+
+    for d in range(D):
+        last = d == D - 1
+        win = T["win%d" % d]
+        add(pl, "x", None, [], ["slots%d" % d], ext=("arr%d" % d, n_arr))
+        wk = own(d) + ["slots%d" % d, "offu"]
+
+        def gat(eng, b, c0=0, c1=4):
+            (acp if eng == "a" else cp)(T.gth[:, 512 * b + 128 * c0:512 * b + 128 * c1],
+                                        win[:, 0:W].indirect(T.offu[:, 32 * b + 8 * c0:32 * b + 8 * c1]), wk,
+                                        ["g%d_%d" % (b, c) for c in range(c0, c1, 2)])
+
+        def press(b):
+            bank, o = (("p0", b) if b < 4 else ("p1", b - 4) if b < 6 else ("p2", b - 6))
+            pe([(T[bank][:, 128 * o:128 * o + 128], T.gth[:, 512 * b + 128 * c:512 * b + 128 * c + 128], T.ident[:],
+                 c == 0, c == 3) for c in range(4)], ["g%d_0" % b, "g%d_2" % b, "ident"], [bank])
+
+        def best(bank, c0, n):
+            tt(T.sc[:, c0:c0 + n], T[bank][:, 0:n], T.st[:, c0:c0 + n], A.mult, [bank, "st0", "st1"], ["sc" + bank])
+            v(lambda: V.tensor_tensor_scan(T.kk[:, c0:c0 + n], T.d0[:, 0:n], T.sc[:, c0:c0 + n], 0.0, A.add, A.max),
+              ["d0", "sc" + bank], ["kk" + bank])
+
+        def event(s, banks):
+            j0 = 32 * s
+            nm = "AB"[s]
+            ts(T.ki[:, j0:j0 + 32], T.kk[:, 16 * j0 + 15:16 * j0 + 512:16], float(32 * TH + 16), None, A.max, None,
+               ["kk" + b for b in banks], ["ki" + nm])
+            ts(T.ri[:, j0:j0 + 32], T.ki[:, j0:j0 + 32], 31, None, A.bitwise_and, None, ["ki" + nm], ["ri" + nm])
+            cp(T.ee[:, 2 * j0:2 * j0 + 64:2], T.ri[:, j0:j0 + 32], ["ri" + nm], ["e" + nm])
+            tt(T.ee[:, 2 * j0 + 1:2 * j0 + 64:2], T.ri[:, j0:j0 + 32], T.ri[:, j0:j0 + 32], A.mult, ["ri" + nm], ["q" + nm])
+            v(lambda: V.transpose(T.et[:, 2 * j0:2 * j0 + 64], T.ee[:, 2 * j0:2 * j0 + 64]), ["e" + nm, "q" + nm], ["et" + nm])
+
+        def spread(zn, b0, b1, nm):
+            mm = []
+            for b in range(b0, b1):
+                for k in range(4):
+                    o = 128 * (b - b0) + 32 * k
+                    w0 = 256 * k + 128 * (b % 2)
+                    mm.append((T[zn][:, o:o + 32], T.wz[:, w0:w0 + 128], T.et[:, 32 * (b // 2):32 * (b // 2) + 32],
+                               False, b == b1 - 1 and k == 3))
+            pe(mm, ["wq0", "wq1", "wq2", "wq3", "et" + nm], [zn])
+
+        def fresh(zn, c0, n, key):
+            out = T.ybuf if last else T["win%d" % (d + 1)]
+            tt(out[:, c0:c0 + n], T[zn][:, 0:n], T.half[:, c0:c0 + n], A.max, [zn, "half"], [key + str(d + 1)])
+            if last:
+                load("s", T.y[:, c0:c0 + n], T.ybuf[:, c0:c0 + n], [key + str(d + 1)], ["y" + key])
+
+        gat("a", 0)
+        gat("v", 2)
+        gat("a", 1)
+        gat("v", 3)
+        gat("a", 4)
+        gat("v", 5, 0, 2)
+        gat("a", 5, 2, 4)
+        gat("a", 6)
+        gat("a", 7)
+        for b in (0, 2, 1, 3, 4, 5):
+            press(b)
+        best("p0", 0, 512)
+        event(0, ["p0"])
+        press(6)
+        spread("z0", 0, 4, "A")
+        best("p1", 512, 256)
+        press(7)
+        fresh("z0", 0, 512, "oA")
+        best("p2", 768, 256)
+        event(1, ["p1", "p2"])
+        spread("z1", 4, 6, "B")
+        spread("z2", 6, 8, "B")
+        early = 8 if last else EARLY_MASKS
+        masks(0, early)
+        fresh("z1", 512, 256, "oB")
+        fresh("z2", 768, 256, "oC")
+        if last:
+            fix()
+            history()
+            cp(T.hout[:], T.cf[:].indirect(T.pmu[:, 32:36]), ["cf", "pm64"], ["hout"])
+            load("a", T.h[:], T.hout[:], ["hout"], ["h"])
+            add(pl, "s", None, ["yoA", "yoB", "yoC", "h"], [])
+            break
+        gather_shown(d + 1, "a", 0, 2)
+        gather_shown(d + 1, "v", 2, 4)
+        send_far(d + 1)
+        masks(early, 8)
+        fix()
+        gather_shown(d + 1, "v", 4, 6)
+        gather_shown(d + 1, "a", 6, 7)
+        send_near(d + 1, [0, 1])
+        send_near(d + 1, [2])
+        history()
+        cp(T.cu[:], T.cf[:].indirect(T.pmu[:, 32:36]), ["cf", "pm64"], ["cu"])
+        suscept()
+        tt(T.tmpo[:], T.hit[:].indirect(T.pmu[:, 16:32]), T.dif[:], A.mult, ["hit", "pmI", "dif"], ["tmpo"])
+        tt(T.offf[:], T.tmpo[:], T.homf[:], A.add, ["tmpo", "homf"], ["offf"])
+        cp(T.offu[:], T.offf[:], ["offf"], ["offu"])
+        halves(d + 1)
+        next_code()
+    emit(pl, queues, T)
+    g.wait_ge(T.sem.sent, sent[0])

@@ -3,7 +3,7 @@ from concourse.mybir import AluOpType, ActivationFunctionType
 
 P, S, D, TH = 1024, 160, 3, 11008
 W = P + 7 * S
-NSEM = 60
+NSEM = 70
 BF, F32, I32, U16 = "bfloat16", "float32", "int32", "uint16"
 SCRATCH = {}
 for _d in range(D):
@@ -15,19 +15,19 @@ for _n, _c, _t in (
         ("hsi", 64, I32), ("cf", 64, F32), ("cu", 64, U16), ("ci", 64, I32), ("c7", 64, I32), ("ct", 64, F32), ("af", 64, F32),
         ("hit", 64, F32), ("uu", 64, F32), ("tt", 64, F32), ("hout", 64, F32),
         ("gth", 4096, BF), ("sg", P, BF), ("st", P, BF), ("sc", P, F32), ("kk", P, F32), ("ki", 64, I32), ("ri", 64, I32),
-        ("ee", 128, BF), ("et", 128, BF), ("rr", 512, BF), ("hy", P, BF), ("half", P, BF),
-        ("ident", 128, BF), ("d0", 512, BF), ("wz0", 256, BF), ("wz", 1024, BF), ("m4", 4, F32), ("dg", 128, BF),
-        ("ones", 512, BF), ("mk", 8, F32),
-        ("wd", 240, BF), ("pci", 8, I32), ("pcf", 8, F32), ("pd", 8, F32), ("cc", 240, F32), ("pmf", 36, F32), ("pmu", 36, U16),
-        ("ia", 256, F32), ("ib", 256, F32), ("wa", 256, F32), ("wb", 256, F32)):
+        ("ee", 256, BF), ("et", 256, BF), ("rr", 512, BF), ("hy", P, BF), ("half", P, BF),
+        ("ident", 128, BF), ("d0", 512, BF), ("wz0", 128, BF), ("wz", 512, BF), ("m4", 4, F32), ("mk", 8, F32),
+        ("wd", 240, BF), ("pci", 10, I32), ("pcf", 10, F32), ("pd", 16, F32), ("cc", 240, F32), ("pmf", 32, F32), ("pmu", 40, U16),
+        ("ia", 128, F32), ("ib", 128, F32), ("wa", 128, F32), ("wb", 128, F32), ("wc", 128, F32), ("we", 128, F32)):
     SCRATCH[_n] = ("sbuf", [128, _c], _t)
-for _n in ("p0", "p1", "p2", "z0", "z1", "z2", "fx"):
+for _n in ("p0", "p1", "p2", "p3", "z0", "z1", "z2", "fx"):
     SCRATCH[_n] = ("psum", [128, 512], F32)
 SEMAPHORES = ["sent", "arr0", "arr1", "arr2", "rin0", "rin1", "rin2"] + ["s%d" % _i for _i in range(NSEM)]
 
 A = AluOpType
 ACT = ActivationFunctionType
-EARLY_MASKS = 5
+NA = 6
+ZB = (("z0", 0, 384), ("z1", 384, 384), ("z2", 768, 256))
 
 
 def routes(T, topo):
@@ -252,20 +252,25 @@ def rank_program(g, core, T, topo):
     def col(t, j):
         return t[:, j:j + 1]
 
-    def masks(u0, u1):
+    def masks(eng, nm, u0, u1):
+        j0, j1 = {"A": (0, 8 * NA), "B": (8 * NA, 64), "AB": (0, 64)}[nm]
         for u in range(u0, u1):
-            a(lambda u=u: AC.activation(T.rr[:, 64 * u:64 * u + 64], T.ee[:, 0:128:2], ACT.Identity, scale=col(T.mk, u)),
-              ["eA", "eB", "mk"], ["rr%d" % u])
+            out, in_ = T.rr[:, 64 * u + j0:64 * u + j1], T.ee[:, 4 * j0:4 * j1:4]
+            r, w = ["e" + x for x in nm] + ["mk"], ["rr%s%d" % (x, u) for x in nm]
+            if eng == "a":
+                a(lambda out=out, in_=in_, u=u: AC.activation(out, in_, ACT.Identity, scale=col(T.mk, u)), r, w)
+            else:
+                ts(out, in_, col(T.mk, u), None, A.mult, None, r, w)
 
     def fix():
         pe([(T.fx[:, 0:64], T.wd[:, 112 - 16 * k:240 - 16 * k], T.rr[:, k:512:8], k == 0, k == 7) for k in range(8)],
-           ["wd"] + ["rr%d" % u for u in range(8)], ["fx"])
+           ["wd"] + ["rr%s%d" % (nm, u) for nm in "AB" for u in range(8)], ["fx"])
 
-    def history():
+    def history(out, key):
         ts(T.hit[:], T.fx[:, 0:64], 16.0, None, A.is_lt, None, ["fx"], ["hit"])
         tt(T.uu[:], T.af[:], T.fx[:, 0:64], A.subtract, ["af", "fx"], ["uu"])
         tt(T.tt[:], T.uu[:], T.hit[:], A.mult, ["uu", "hit"], ["tt"])
-        tt(T.cf[:], T.tt[:], T.cf[:], A.add, ["tt", "cf"], ["cf"])
+        tt(out, T.tt[:], T.cf[:], A.add, ["tt", "cf", "pmN"], [key])
 
     def suscept():
         for k in range(2):
@@ -282,9 +287,8 @@ def rank_program(g, core, T, topo):
     def halves(d):
         ts(T.hy[:], T["win%d" % d][:, 0:P], 0.5, 127.8, A.mult, A.add, own(d), ["hy"])
         ts(T.half[:], T.hy[:], 128.0, None, A.subtract, None, ["hy"], ["half"])
-        for zn, c0, n in (("z0", 0, 512), ("z1", 512, 256), ("z2", 768, 256)):
-            pe([(T[zn][:, 0:n], T.ident[:], T.half[:, c0:c0 + n], True, False),
-                (T[zn][:, 0:n], T.dg[:], T.ones[:, 0:n], False, False)], ["ident", "half", "dg", "ones"], [zn])
+        for zn, c0, n in ZB:
+            pe([(T[zn][:, 0:n], T.ident[:], T.half[:, c0:c0 + n], True, False)], ["ident", "half"], [zn])
 
     def next_code():
         cp(T.ci[:], T.cf[:], ["cf"], ["ci"])
@@ -299,63 +303,72 @@ def rank_program(g, core, T, topo):
     load("s", T.homi[:], T.home[:], [], ["homi"])
     load("s", T.awyi[:], T.away[:], [], ["awyi"])
     iota(col(T.pci, 6), [[0, 1]], 0, 1, ["pi"], flt=False)
-    iota(T.pmf[:, 0:16], [[8, 8], [128, 2]], 0, 0, ["pmf0"])
+    iota(T.pmf[:, 0:16], [[2, 8], [128, 2]], 0, 0, ["pmf0"])
     iota(T.pmf[:, 16:32], [[1, 8], [0, 2]], 0, 0, ["pmf1"])
-    iota(T.pmf[:, 32:36], [[2, 4]], 0, 0, ["pmf2"])
     iota(T.cc[:], [[1, 240]], 0, 0, ["cc"])
     v(lambda: V.memset(T.d0[:], 1.0), [], ["d0"])
-    v(lambda: V.memset(T.ones[:], 1.0), [], ["ones"])
+    v(lambda: V.memset(T.ee[:], 1.0), [], ["eA", "qA", "eB", "qB"])
+    v(lambda: V.memset(T.hout[:], 0.0), [], ["hout"])
     v(lambda: V.memset(T.d0[:, 0:512:16], -3.0e7), [], ["d0"])
     pi = col(T.pci, 6)
     ts(col(T.pci, 0), pi, 7, None, A.bitwise_and, None, ["pi"], ["pc0"])
     ts(col(T.pci, 1), pi, 3, 1, A.arith_shift_right, A.bitwise_and, ["pi"], ["pc1"])
     ts(col(T.pci, 2), pi, 15, None, A.bitwise_and, None, ["pi"], ["pc2"])
     ts(col(T.pci, 3), pi, 4, None, A.arith_shift_right, None, ["pi"], ["pc3"])
-    ts(col(T.pci, 4), pi, 1, None, A.bitwise_and, None, ["pi"], ["pc4"])
-    ts(col(T.pci, 5), pi, 31, 1, A.bitwise_and, A.arith_shift_right, ["pi"], ["pc5"])
+    ts(col(T.pci, 4), pi, 3, None, A.bitwise_and, None, ["pi"], ["pc4"])
+    ts(col(T.pci, 5), pi, 31, 2, A.bitwise_and, A.arith_shift_right, ["pi"], ["pc5"])
     ts(col(T.pci, 7), pi, 5, None, A.arith_shift_right, None, ["pi"], ["pc6"])
-    conv_shown(0, 4)
+    ts(col(T.pci, 8), pi, 1, None, A.bitwise_and, None, ["pi"], ["pc7"])
+    ts(col(T.pci, 9), pi, 6, None, A.bitwise_and, None, ["pi"], ["pc8"])
+    cp(T.pcf[:], T.pci[:], ["pi"] + ["pc%d" % j for j in range(9)], ["pcf"])
+    conv_shown(0, 7)
     gather_shown(0, "a", 0, 2)
     gather_shown(0, "v", 2, 4)
     send_far(0)
-    conv_shown(4, 7)
     gather_shown(0, "a", 4, 6)
     gather_shown(0, "v", 6, 7)
     send_near(0, [0, 1])
     send_near(0, [2])
-    iota(T.ia[:], [[1, 16], [0, 16]], 0, 0, ["ia"])
-    iota(T.ib[:], [[0, 16], [-1, 16]], 15, 0, ["ib"])
-    cp(T.cu[:], T.hsi[:], ["hsi"], ["cu"])
-    cp(T.pcf[:], T.pci[:], ["pi"] + ["pc%d" % j for j in range(7)], ["pcf"])
-    a7, hh, q16, uc, kd, q32, pf, quad = [col(T.pcf, j) for j in range(8)]
+    iota(T.ia[:], [[1, 8], [0, 16]], 0, 0, ["ia"])
+    iota(T.ib[:], [[0, 8], [-1, 16]], 15, 0, ["ib"])
+    a7, hh, q16, uc, f4, g8, pf, quad, b1, a6 = [col(T.pcf, j) for j in range(10)]
+    pd = [col(T.pd, j) for j in range(16)]
+    ts(pd[0], a7, float(NA), None, A.is_ge, None, ["pcf"], ["pd0"])
+    ts(pd[1], a7, 2.0, hh, A.mult, A.add, ["pcf"], ["pd1"])
+    ts(pd[2], hh, 64.0, b1, A.mult, A.add, ["pcf"], ["pd2"])
+    ts(pd[7], a7, 8.0, hh, A.mult, A.add, ["pcf"], ["pd7"])
+    ts(pd[3], pd[0], 16.0 - 4 * NA, 2.0 * NA, A.mult, A.add, ["pd0"], ["pd3"])
+    ts(pd[4], pd[0], 6.0 * NA, pd[1], A.mult, A.add, ["pd0", "pd1"], ["pd4"])
+    ts(pd[5], a6, float(NA), pd[2], A.mult, A.add, ["pcf", "pd2"], ["pd5"])
+    ts(pd[6], a6, 8.0 - NA, pd[2], A.mult, A.add, ["pcf", "pd2"], ["pd6"])
+    ts(T.pmu[:, 32:36], T.cc[:, 0:8:2], pd[7], None, A.add, None, ["cc", "pd7"], ["pm64"])
+    ts(T.pmu[:, 36:40], T.cc[:, 0:4], pd[3], pd[4], A.mult, A.add, ["cc", "pd3", "pd4"], ["pmN"])
+    ts(T.pmu[:, 0:2 * NA], T.pmf[:, 0:2 * NA], pd[5], None, A.add, None, ["pmf0", "pd5"], ["pmH0"])
+    ts(T.pmu[:, 2 * NA:16], T.pmf[:, 2 * NA:16], pd[6], 6.0 * NA, A.add, A.add, ["pmf0", "pd6"], ["pmH"])
+    cp(T.cf[:], T.hsi[:].indirect(T.pmu[:, 36:40]), ["hsi", "pmN"], ["cf"])
     ts(T.ident[:], T.cc[:, 0:128], pf, None, A.is_equal, None, ["cc", "pcf"], ["ident"])
-    ts(col(T.pd, 0), a7, 8.0, hh, A.mult, A.add, ["pcf"], ["pd0"])
-    ts(col(T.pd, 1), a7, 8.0, None, A.mult, None, ["pcf"], ["pd1"])
-    ts(col(T.pd, 2), hh, 64.0, a7, A.mult, A.add, ["pcf"], ["pd2"])
-    ts(col(T.pd, 3), kd, -128.0, 128.0, A.mult, A.add, ["pcf"], ["pd3"])
-    ts(col(T.pd, 4), kd, -64.0, None, A.mult, None, ["pcf"], ["pd4"])
-    ts(col(T.pd, 5), q16, 15.0, None, A.subtract, None, ["pcf"], ["pd5"])
-    ts(T.pmu[:, 0:16], T.pmf[:, 0:16], col(T.pd, 2), None, A.add, None, ["pmf0", "pd2"], ["pmH"])
-    ts(T.pmu[:, 16:32], T.pmf[:, 16:32], col(T.pd, 1), None, A.add, None, ["pmf1", "pd1"], ["pmI"])
-    ts(T.pmu[:, 32:36], T.pmf[:, 32:36], col(T.pd, 0), None, A.add, None, ["pmf2", "pd0"], ["pm64"])
-    ts(col(T.pd, 6), col(T.pd, 5), col(T.pd, 5), -64.0, A.mult, A.mult, ["pd5"], ["pd6"])
-    cp(T.offu[:], T.homi[:].indirect(T.pmu[:, 0:16]), ["homi", "pmH"], ["offu"])
-    ts(col(T.pd, 7), col(T.pd, 6), 64.0, None, A.add, None, ["pd6"], ["pd7"])
+    cp(T.cu[:], T.cf[:].indirect(T.pmu[:, 32:36]), ["cf", "pm64"], ["cu"])
+    cp(T.offu[:], T.homi[:].indirect(T.pmu[:, 0:16]), ["homi", "pmH0", "pmH"], ["offu"])
     suscept()
-    ts(T.dg[:], T.ident[:], col(T.pd, 7), None, A.mult, None, ["ident", "pd7"], ["dg"])
     halves(0)
-    ts(T.wa[:], T.ia[:], q32, None, A.is_equal, None, ["ia", "pcf"], ["wa"])
-    ts(T.wb[:], T.ib[:], col(T.pd, 3), col(T.pd, 4), A.mult, A.add, ["ib", "pd3", "pd4"], ["wb"])
+    ts(pd[8], a7, 8.0, None, A.mult, None, ["pcf"], ["pd8"])
+    ts(pd[9], f4, 0.0, 128.0, A.is_equal, A.mult, ["pcf"], ["pd9"])
+    ts(pd[10], f4, 2.0, -64.0, A.is_equal, A.mult, ["pcf"], ["pd10"])
+    ts(pd[11], f4, 1.0, -64.0, A.is_equal, A.mult, ["pcf"], ["pd11"])
+    ts(T.pmu[:, 16:32], T.pmf[:, 16:32], pd[8], None, A.add, None, ["pmf1", "pd8"], ["pmI"])
+    ts(T.wb[:], T.ib[:], pd[10], pd[9], A.mult, A.add, ["ib", "pd9", "pd10"], ["wb"])
+    ts(T.wa[:], T.ia[:], g8, None, A.is_equal, None, ["ia", "pcf"], ["wa"])
     ts(T.mk[:], T.cc[:, 0:8], uc, None, A.is_equal, None, ["cc", "pcf"], ["mk"])
+    tt(T.wc[:], T.wb[:], T.ib[:], A.mult, ["wb", "ib"], ["wc"])
     ts(T.m4[:], T.cc[:, 0:4], quad, None, A.is_equal, None, ["cc", "pcf"], ["m4"])
-    tt(T.wz0[:], T.wa[:], T.wb[:], A.mult, ["wa", "wb"], ["wz0"])
+    ts(T.we[:], T.wc[:], pd[11], pd[10], A.add, A.subtract, ["wc", "pd10", "pd11"], ["we"])
     ts(T.wd[:], T.cc[:], 112.0, q16, A.subtract, A.is_equal, ["cc", "pcf"], ["wd"])
+    tt(T.wz0[:], T.wa[:], T.we[:], A.mult, ["wa", "we"], ["wz0"])
+    cp(T.homf[:], T.homi[:].indirect(T.pmu[:, 0:16]), ["homi", "pmH0", "pmH"], ["homf"])
     for k in range(4):
-        ts(T.wz[:, 256 * k:256 * k + 256], T.wz0[:], col(T.m4, k), None, A.mult, None, ["wz0", "m4"], ["wq%d" % k])
-    cp(T.cf[:], T.hsi[:].indirect(T.pmu[:, 32:36]), ["hsi", "pm64"], ["cf"])
-    cp(T.homf[:], T.homi[:].indirect(T.pmu[:, 0:16]), ["homi", "pmH"], ["homf"])
+        ts(T.wz[:, 128 * k:128 * k + 128], T.wz0[:], col(T.m4, k), None, A.mult, None, ["wz0", "m4"], ["wq%d" % k])
+    cp(T.awyf[:], T.awyi[:].indirect(T.pmu[:, 0:16]), ["awyi", "pmH0", "pmH"], ["awyf"])
     next_code()
-    cp(T.awyf[:], T.awyi[:].indirect(T.pmu[:, 0:16]), ["awyi", "pmH"], ["awyf"])
     tt(T.dif[:], T.awyf[:], T.homf[:], A.subtract, ["awyf", "homf"], ["dif"])
 
     for d in range(D):
@@ -367,93 +380,106 @@ def rank_program(g, core, T, topo):
         def gat(eng, b, c0=0, c1=4):
             (acp if eng == "a" else cp)(T.gth[:, 512 * b + 128 * c0:512 * b + 128 * c1],
                                         win[:, 0:W].indirect(T.offu[:, 32 * b + 8 * c0:32 * b + 8 * c1]), wk,
-                                        ["g%d_%d" % (b, c) for c in range(c0, c1, 2)])
+                                        ["g%d_%d" % (b, c) for c in range(c0, c1)])
 
-        def press(b):
-            bank, o = (("p0", b) if b < 4 else ("p1", b - 4) if b < 6 else ("p2", b - 6))
+        def press(b, c0=0, c1=4):
+            bank, o = (("p0", b) if b < 4 else ("p1", b - 4) if b < 6 else ("p%d" % (b - 4), 0))
             pe([(T[bank][:, 128 * o:128 * o + 128], T.gth[:, 512 * b + 128 * c:512 * b + 128 * c + 128], T.ident[:],
-                 c == 0, c == 3) for c in range(4)], ["g%d_0" % b, "g%d_2" % b, "ident"], [bank])
+                 c == 0, c == 3) for c in range(c0, c1)], ["g%d_%d" % (b, c) for c in range(c0, c1)] + ["ident"], [bank])
+
+        def score(bank, c0, n):
+            tt(T.sc[:, c0:c0 + n], T[bank][:, 0:n], T.st[:, c0:c0 + n], A.mult, [bank, "st0", "st1"], ["sc" + bank])
 
         def best(bank, c0, n):
-            tt(T.sc[:, c0:c0 + n], T[bank][:, 0:n], T.st[:, c0:c0 + n], A.mult, [bank, "st0", "st1"], ["sc" + bank])
             v(lambda: V.tensor_tensor_scan(T.kk[:, c0:c0 + n], T.d0[:, 0:n], T.sc[:, c0:c0 + n], 0.0, A.add, A.max),
               ["d0", "sc" + bank], ["kk" + bank])
 
-        def event(s, banks):
-            j0 = 32 * s
-            nm = "AB"[s]
-            ts(T.ki[:, j0:j0 + 32], T.kk[:, 16 * j0 + 15:16 * j0 + 512:16], float(32 * TH + 16), None, A.max, None,
-               ["kk" + b for b in banks], ["ki" + nm])
-            ts(T.ri[:, j0:j0 + 32], T.ki[:, j0:j0 + 32], 31, None, A.bitwise_and, None, ["ki" + nm], ["ri" + nm])
-            cp(T.ee[:, 2 * j0:2 * j0 + 64:2], T.ri[:, j0:j0 + 32], ["ri" + nm], ["e" + nm])
-            tt(T.ee[:, 2 * j0 + 1:2 * j0 + 64:2], T.ri[:, j0:j0 + 32], T.ri[:, j0:j0 + 32], A.mult, ["ri" + nm], ["q" + nm])
-            v(lambda: V.transpose(T.et[:, 2 * j0:2 * j0 + 64], T.ee[:, 2 * j0:2 * j0 + 64]), ["e" + nm, "q" + nm], ["et" + nm])
+        def event(nm, step):
+            j0, j1, banks = (0, 8 * NA, ["p0", "p1"]) if nm == "A" else (8 * NA, 64, ["p2", "p3"])
+            if step == 0:
+                ts(T.ki[:, j0:j1], T.kk[:, 16 * j0 + 15:16 * j1:16], float(32 * TH + 16), None, A.max, None,
+                   ["kk" + b for b in banks], ["ki" + nm])
+            elif step == 1:
+                ts(T.ri[:, j0:j1], T.ki[:, j0:j1], 31, None, A.bitwise_and, None, ["ki" + nm], ["ri" + nm])
+            elif step == 2:
+                cp(T.ee[:, 4 * j0:4 * j1:4], T.ri[:, j0:j1], ["ri" + nm], ["e" + nm])
+                tt(T.ee[:, 4 * j0 + 1:4 * j1:4], T.ri[:, j0:j1], T.ri[:, j0:j1], A.mult, ["ri" + nm], ["q" + nm])
+            else:
+                v(lambda: V.transpose(T.et[:, 4 * j0:4 * j1], T.ee[:, 4 * j0:4 * j1]), ["e" + nm, "q" + nm], ["et" + nm])
 
-        def spread(zn, b0, b1, nm):
-            mm = []
-            for b in range(b0, b1):
-                for k in range(4):
-                    o = 128 * (b - b0) + 32 * k
-                    w0 = 256 * k + 128 * (b % 2)
-                    mm.append((T[zn][:, o:o + 32], T.wz[:, w0:w0 + 128], T.et[:, 32 * (b // 2):32 * (b // 2) + 32],
-                               False, b == b1 - 1 and k == 3))
-            pe(mm, ["wq0", "wq1", "wq2", "wq3", "et" + nm], [zn])
+        def spread(zn, k0, k1, nm):
+            c0, n = (0, 32 * NA) if nm == "A" else (32 * NA, 256 - 32 * NA)
+            pe([(T[zn][:, n * (k - k0):n * (k - k0) + n], T.wz[:, 128 * k:128 * k + 128], T.et[:, c0:c0 + n], False, k == k1 - 1)
+                for k in range(k0, k1)], ["wq0", "wq1", "wq2", "wq3", "et" + nm], [zn])
 
-        def fresh(zn, c0, n, key):
+        def fresh(i):
+            zn, c0, n = ZB[i]
+            key = own(d + 1)[i]
             out = T.ybuf if last else T["win%d" % (d + 1)]
-            tt(out[:, c0:c0 + n], T[zn][:, 0:n], T.half[:, c0:c0 + n], A.max, [zn, "half"], [key + str(d + 1)])
+            tt(out[:, c0:c0 + n], T[zn][:, 0:n], T.half[:, c0:c0 + n], A.max, [zn, "half"], [key])
             if last:
-                load("s", T.y[:, c0:c0 + n], T.ybuf[:, c0:c0 + n], [key + str(d + 1)], ["y" + key])
+                load("s", T.y[:, c0:c0 + n], T.ybuf[:, c0:c0 + n], [key], ["y%d" % i])
 
-        gat("a", 0)
-        gat("v", 2)
-        gat("a", 1)
-        gat("v", 3)
-        gat("a", 4)
-        gat("v", 5, 0, 2)
-        gat("a", 5, 2, 4)
-        gat("a", 6)
-        gat("a", 7)
-        for b in (0, 2, 1, 3, 4, 5):
+        for eng, b in (("a", 2), ("v", 0), ("a", 3), ("v", 1), ("a", 5), ("v", 4), ("a", 6)):
+            gat(eng, b)
+        gat("a", 7, 0, 3)
+        gat("a", 7, 3, 4)
+        for b in (0, 2, 1, 3, 4, 5, 6):
             press(b)
+        press(7, 0, 3)
+        press(7, 3, 4)
+        score("p0", 0, 512)
         best("p0", 0, 512)
-        event(0, ["p0"])
-        press(6)
-        spread("z0", 0, 4, "A")
+        score("p1", 512, 256)
         best("p1", 512, 256)
-        press(7)
-        fresh("z0", 0, 512, "oA")
-        best("p2", 768, 256)
-        event(1, ["p1", "p2"])
-        spread("z1", 4, 6, "B")
-        spread("z2", 6, 8, "B")
-        early = 8 if last else EARLY_MASKS
-        masks(0, early)
-        fresh("z1", 512, 256, "oB")
-        fresh("z2", 768, 256, "oC")
+        score("p2", 768, 128)
+        event("A", 0)
+        best("p2", 768, 128)
+        event("A", 1)
+        score("p3", 896, 128)
+        event("A", 2)
+        best("p3", 896, 128)
+        event("A", 3)
+        spread("z0", 0, 2, "A")
+        spread("z1", 2, 4, "A")
         if last:
+            masks("a", "A", 0, 8)
+        event("B", 0)
+        event("B", 1)
+        event("B", 2)
+        event("B", 3)
+        spread("z2", 0, 4, "B")
+        if last:
+            masks("a", "B", 0, 4)
+            masks("v", "B", 4, 8)
             fix()
-            history()
-            cp(T.hout[:], T.cf[:].indirect(T.pmu[:, 32:36]), ["cf", "pm64"], ["hout"])
+            fresh(0)
+            fresh(1)
+            fresh(2)
+            history(T.hout[:].indirect(T.pmu[:, 36:40]), "hout")
             load("a", T.h[:], T.hout[:], ["hout"], ["h"])
-            add(pl, "s", None, ["yoA", "yoB", "yoC", "h"], [])
+            add(pl, "s", None, ["y0", "y1", "y2", "h"], [])
             break
+        masks("a", "AB", 0, 4)
+        fresh(0)
+        fresh(1)
+        fresh(2)
         gather_shown(d + 1, "a", 0, 2)
         gather_shown(d + 1, "v", 2, 4)
         send_far(d + 1)
-        masks(early, 8)
-        fix()
         gather_shown(d + 1, "v", 4, 6)
         gather_shown(d + 1, "a", 6, 7)
         send_near(d + 1, [0, 1])
         send_near(d + 1, [2])
-        history()
+        masks("a", "AB", 4, 8)
+        fix()
+        halves(d + 1)
+        history(T.cf[:], "cf")
         cp(T.cu[:], T.cf[:].indirect(T.pmu[:, 32:36]), ["cf", "pm64"], ["cu"])
         suscept()
         tt(T.tmpo[:], T.hit[:].indirect(T.pmu[:, 16:32]), T.dif[:], A.mult, ["hit", "pmI", "dif"], ["tmpo"])
         tt(T.offf[:], T.tmpo[:], T.homf[:], A.add, ["tmpo", "homf"], ["offf"])
         cp(T.offu[:], T.offf[:], ["offf"], ["offu"])
-        halves(d + 1)
         next_code()
     emit(pl, queues, T)
     g.wait_ge(T.sem.sent, sent[0])

@@ -16,18 +16,25 @@ for _n, _c, _t in (
         ("hit", 64, F32), ("uu", 64, F32), ("tt", 64, F32), ("hout", 64, F32),
         ("gth", 4096, BF), ("sg", P, BF), ("st", P, BF), ("sc", P, F32), ("kk", P, F32), ("ki", 64, I32), ("ri", 64, I32),
         ("ee", 256, BF), ("et", 256, BF), ("rr", 512, BF), ("hy", P, BF), ("half", P, BF),
-        ("ident", 128, BF), ("d0", 512, BF), ("wz0", 128, BF), ("wz", 512, BF), ("m4", 4, F32), ("mk", 8, F32),
+        ("ident", 128, BF), ("d0", 256, BF), ("wz0", 128, BF), ("wz", 512, BF), ("m4", 4, F32), ("mk", 8, F32),
         ("wd", 240, BF), ("pci", 10, I32), ("pcf", 10, F32), ("pd", 16, F32), ("cc", 240, F32), ("pmf", 32, F32), ("pmu", 40, U16),
         ("ia", 128, F32), ("ib", 128, F32), ("wa", 128, F32), ("wb", 128, F32), ("wc", 128, F32), ("we", 128, F32)):
     SCRATCH[_n] = ("sbuf", [128, _c], _t)
-for _n in ("p0", "p1", "p2", "p3", "z0", "z1", "z2", "fx"):
+NA = 6
+PB = (2, 2, 2, 1, 1)
+ZB = (("z0", 0, 384), ("z1", 384, 384), ("z2", 768, 256))
+GV = ((0, 0, 4), (2, 0, 4), (4, 0, 4))
+GA = ((1, 0, 4), (3, 0, 4), (5, 0, 4), (6, 0, 4), (7, 0, 3), (7, 3, 4))
+FAR_CALLS = ((0, 1), (2, 3))
+DAY = "S0 S1 B0 S2 B1 B2 S3 A0 B3 A1 S4 A2 B4 A3 ZA E0 E1 E2 M F0 E3 ZE X F1 F2"
+LAST = "S0 S1 B0 S2 B1 B2 S3 A0 B3 A1 S4 A2 B4 A3 ZA MA E0 E1 E2 MB F0 E3 ZE X F1 F2 H0 H1 H3"
+BETWEEN = "H0 H1 H2 U0 U1 U2 Ta0 Ta1 O0 N0 L0 N1 O1 N2 O2 N3 L1"
+for _n in ["p%d" % _i for _i in range(len(PB))] + [_z[0] for _z in ZB]:
     SCRATCH[_n] = ("psum", [128, 512], F32)
 SEMAPHORES = ["sent", "arr0", "arr1", "arr2", "rin0", "rin1", "rin2"] + ["s%d" % _i for _i in range(NSEM)]
 
 A = AluOpType
 ACT = ActivationFunctionType
-NA = 6
-ZB = (("z0", 0, 384), ("z1", 384, 384), ("z2", 768, 256))
 
 
 def routes(T, topo):
@@ -136,7 +143,7 @@ def emit(pl, queues, T):
 def helper_program(g, core, T, topo, r, q):
     cores = list(T.cores)
     rid, pid = topo.addr(cores[q], core)
-    n_in = len(topo.engines(cores[r], core)) // 4
+    n_in = len(topo.engines(cores[r], core)) // len(FAR_CALLS[0])
     e = topo.engines(core, cores[q])
     for d in range(D):
         g.wait_ge(T.sem["rin%d" % d], n_in)
@@ -208,7 +215,7 @@ def rank_program(g, core, T, topo):
             add(pl, "g", lambda: g.iota(out, pat, base, cm), [], w)
 
     def own(d):
-        return ["oA%d" % d, "oB%d" % d, "oC%d" % d]
+        return ["o%d_%d" % (i, d) for i in range(len(ZB))]
 
     def conv_shown(t0, t1):
         for t in range(t0, t1):
@@ -221,18 +228,33 @@ def rank_program(g, core, T, topo):
         (acp if eng == "a" else cp)(T["snd%d" % d][:, S * t0:S * t1], src, own(d) + ["shu%d" % t for t in range(t0, t1)],
                                     ["snd%d_%d" % (d, t) for t in range(t0, t1)])
 
-    def send_far(d):
+    def send_far(d, ts_):
         def fn():
             trs = []
-            for t, (q, h) in enumerate(far):
+            for i, t in enumerate(ts_):
+                q, h = far[t]
                 rid, pid = topo.addr(h, core)
-                e = topo.engines(core, h)[t::len(far)]
+                e = topo.engines(core, h)[i::len(ts_)]
                 trs.append(RemoteDMATransfer(dst_ids=[DstId(rid=rid, pnc=pid)], dma_engine_mask=bits(e),
                                              remote_sem=T.sem["rin%d" % d], src=T["snd%d" % d][:, S * t:S * t + S],
                                              dst=T["snd%d" % d][:, 0:S]))
                 sent[0] += len(e)
             return g.remote_dma_fused(trs, local_sem=T.sem.sent)
-        add(pl, "g", fn, ["snd%d_%d" % (d, t) for t in range(4)], [])
+        add(pl, "g", fn, ["snd%d_%d" % (d, t) for t in ts_], [])
+
+    def exchange(d):
+        for ts_ in FAR_CALLS:
+            h = len(ts_) // 2
+            gather_shown(d, "a", ts_[0], ts_[0] + h)
+            gather_shown(d, "v", ts_[h], ts_[h] + h)
+            send_far(d, ts_)
+        gather_shown(d, "a", 4, 6)
+        if d == 0:
+            gather_shown(d, "v", 6, 7)
+        else:
+            gather_shown(d, "a", 6, 7)
+        send_near(d, [0, 1])
+        send_near(d, [2])
 
     def send_near(d, js):
         def fn():
@@ -263,38 +285,67 @@ def rank_program(g, core, T, topo):
                 ts(out, in_, col(T.mk, u), None, A.mult, None, r, w)
 
     def fix():
-        pe([(T.fx[:, 0:64], T.wd[:, 112 - 16 * k:240 - 16 * k], T.rr[:, k:512:8], k == 0, k == 7) for k in range(8)],
-           ["wd"] + ["rr%s%d" % (nm, u) for nm in "AB" for u in range(8)], ["fx"])
+        pe([(T.p0[:, 0:64], T.wd[:, 112 - 16 * k:240 - 16 * k], T.rr[:, k:512:8], k == 0, k == 7) for k in range(8)],
+           ["wd"] + ["rr%s%d" % (nm, u) for nm in "AB" for u in range(8)], ["p0"])
 
-    def history(out, key):
-        ts(T.hit[:], T.fx[:, 0:64], 16.0, None, A.is_lt, None, ["fx"], ["hit"])
-        tt(T.uu[:], T.af[:], T.fx[:, 0:64], A.subtract, ["af", "fx"], ["uu"])
-        tt(T.tt[:], T.uu[:], T.hit[:], A.mult, ["uu", "hit"], ["tt"])
-        tt(out, T.tt[:], T.cf[:], A.add, ["tt", "cf", "pmN"], [key])
+    def history(j):
+        if j == 0:
+            ts(T.hit[:], T.p0[:, 0:64], 16.0, None, A.is_lt, None, ["p0"], ["hit"])
+            tt(T.uu[:], T.af[:], T.p0[:, 0:64], A.subtract, ["af", "p0"], ["uu"])
+        elif j == 1:
+            tt(T.tt[:], T.uu[:], T.hit[:], A.mult, ["uu", "hit"], ["tt"])
+        elif j == 2:
+            tt(T.cf[:], T.tt[:], T.cf[:], A.add, ["tt", "cf"], ["cf"])
+        else:
+            tt(T.hout[:].indirect(T.pmu[:, 36:40]), T.tt[:], T.cf[:], A.add, ["tt", "cf", "pmN"], ["hout"])
+            load("a", T.h[:], T.hout[:], ["hout"], ["h"])
 
-    def suscept():
-        for k in range(2):
+    def sus_gather(j):
+        if j == 0:
+            cp(T.cu[:], T.cf[:].indirect(T.pmu[:, 32:36]), ["cf", "pm64"], ["cu"])
+        else:
+            k = j - 1
             acp(T.sg[:, 512 * k:512 * k + 512], T.susb[:, 0:2048].indirect(T.cu[:, 32 * k:32 * k + 32]), ["susb", "cu"],
                 ["sg%d" % k], scale=32.0)
-        for k in range(2):
-            pb = T["p%d" % k]
-            for b in range(4):
-                pe([(pb[:, 128 * b:128 * b + 128], T.sg[:, 512 * k + 128 * b:512 * k + 128 * b + 128], T.ident[:], True, True)],
-                   ["sg%d" % k, "ident"], ["p%d" % k])
-        for k in range(2):
-            acp(T.st[:, 512 * k:512 * k + 512], T["p%d" % k][:], ["p%d" % k], ["st%d" % k])
 
-    def halves(d):
-        ts(T.hy[:], T["win%d" % d][:, 0:P], 0.5, 127.8, A.mult, A.add, own(d), ["hy"])
-        ts(T.half[:], T.hy[:], 128.0, None, A.subtract, None, ["hy"], ["half"])
+    def sus_turn(eng, k):
+        bank = "p%d" % (k + 1)
+        for b in range(4):
+            pe([(T[bank][:, 128 * b:128 * b + 128], T.sg[:, 512 * k + 128 * b:512 * k + 128 * b + 128], T.ident[:], True, True)],
+               ["sg%d" % k, "ident"], [bank])
+        (acp if eng == "a" else cp)(T.st[:, 512 * k:512 * k + 512], T[bank][:], [bank], ["st%d" % k])
+
+    def halves(d, j, eng):
+        if j == 0:
+            if eng == "a":
+                a(lambda: AC.activation(T.hy[:], T["win%d" % d][:, 0:P], ACT.Copy, scale=0.5, bias=127.8), own(d), ["hy"])
+            else:
+                ts(T.hy[:], T["win%d" % d][:, 0:P], 0.5, 127.8, A.mult, A.add, own(d), ["hy"])
+            return
+        if eng == "a":
+            a(lambda: AC.activation(T.half[:], T.hy[:], ACT.Copy, bias=-128.0), ["hy"], ["half"])
+        else:
+            ts(T.half[:], T.hy[:], 128.0, None, A.subtract, None, ["hy"], ["half"])
         for zn, c0, n in ZB:
             pe([(T[zn][:, 0:n], T.ident[:], T.half[:, c0:c0 + n], True, False)], ["ident", "half"], [zn])
 
-    def next_code():
-        cp(T.ci[:], T.cf[:], ["cf"], ["ci"])
-        ts(T.c7[:], T.ci[:], 127, None, A.bitwise_and, None, ["ci"], ["c7"])
-        ts(T.ct[:], T.c7[:], 16.0, 15.0, A.mult, A.add, ["c7"], ["ct"])
-        tt(T.af[:], T.ct[:], T.cf[:], A.subtract, ["ct", "cf"], ["af"])
+    def next_code(j):
+        if j == 0:
+            cp(T.ci[:], T.cf[:], ["cf"], ["ci"])
+        elif j == 1:
+            ts(T.c7[:], T.ci[:], 127, None, A.bitwise_and, None, ["ci"], ["c7"])
+        elif j == 2:
+            ts(T.ct[:], T.c7[:], 16.0, 15.0, A.mult, A.add, ["c7"], ["ct"])
+        else:
+            tt(T.af[:], T.ct[:], T.cf[:], A.subtract, ["ct", "cf"], ["af"])
+
+    def contacts(j):
+        if j == 0:
+            tt(T.tmpo[:], T.hit[:].indirect(T.pmu[:, 16:32]), T.dif[:], A.mult, ["hit", "pmI", "dif"], ["tmpo"])
+        elif j == 1:
+            tt(T.offf[:], T.tmpo[:], T.homf[:], A.add, ["tmpo", "homf"], ["offf"])
+        else:
+            cp(T.offu[:], T.offf[:], ["offf"], ["offu"])
 
     load("s", T.win0[:, 0:P], T.x[:], [], own(0))
     load("a", T.shi[:], T.shown[:], [], ["shi"])
@@ -306,10 +357,12 @@ def rank_program(g, core, T, topo):
     iota(T.pmf[:, 0:16], [[2, 8], [128, 2]], 0, 0, ["pmf0"])
     iota(T.pmf[:, 16:32], [[1, 8], [0, 2]], 0, 0, ["pmf1"])
     iota(T.cc[:], [[1, 240]], 0, 0, ["cc"])
+    iota(T.ia[:], [[1, 8], [0, 16]], 0, 0, ["ia"])
+    iota(T.ib[:], [[0, 8], [-1, 16]], 15, 0, ["ib"])
     v(lambda: V.memset(T.d0[:], 1.0), [], ["d0"])
     v(lambda: V.memset(T.ee[:], 1.0), [], ["eA", "qA", "eB", "qB"])
     v(lambda: V.memset(T.hout[:], 0.0), [], ["hout"])
-    v(lambda: V.memset(T.d0[:, 0:512:16], -3.0e7), [], ["d0"])
+    v(lambda: V.memset(T.d0[:, 0:256:16], -3.0e7), [], ["d0"])
     pi = col(T.pci, 6)
     ts(col(T.pci, 0), pi, 7, None, A.bitwise_and, None, ["pi"], ["pc0"])
     ts(col(T.pci, 1), pi, 3, 1, A.arith_shift_right, A.bitwise_and, ["pi"], ["pc1"])
@@ -321,22 +374,17 @@ def rank_program(g, core, T, topo):
     ts(col(T.pci, 8), pi, 1, None, A.bitwise_and, None, ["pi"], ["pc7"])
     ts(col(T.pci, 9), pi, 6, None, A.bitwise_and, None, ["pi"], ["pc8"])
     cp(T.pcf[:], T.pci[:], ["pi"] + ["pc%d" % j for j in range(9)], ["pcf"])
-    conv_shown(0, 7)
-    gather_shown(0, "a", 0, 2)
-    gather_shown(0, "v", 2, 4)
-    send_far(0)
-    gather_shown(0, "a", 4, 6)
-    gather_shown(0, "v", 6, 7)
-    send_near(0, [0, 1])
-    send_near(0, [2])
-    iota(T.ia[:], [[1, 8], [0, 16]], 0, 0, ["ia"])
-    iota(T.ib[:], [[0, 8], [-1, 16]], 15, 0, ["ib"])
     a7, hh, q16, uc, f4, g8, pf, quad, b1, a6 = [col(T.pcf, j) for j in range(10)]
     pd = [col(T.pd, j) for j in range(16)]
+    ts(T.ident[:], T.cc[:, 0:128], pf, None, A.is_equal, None, ["cc", "pcf"], ["ident"])
     ts(pd[0], a7, float(NA), None, A.is_ge, None, ["pcf"], ["pd0"])
     ts(pd[1], a7, 2.0, hh, A.mult, A.add, ["pcf"], ["pd1"])
     ts(pd[2], hh, 64.0, b1, A.mult, A.add, ["pcf"], ["pd2"])
     ts(pd[7], a7, 8.0, hh, A.mult, A.add, ["pcf"], ["pd7"])
+    conv_shown(0, 7)
+    exchange(0)
+    halves(0, 0, "a")
+    halves(0, 1, "a")
     ts(pd[3], pd[0], 16.0 - 4 * NA, 2.0 * NA, A.mult, A.add, ["pd0"], ["pd3"])
     ts(pd[4], pd[0], 6.0 * NA, pd[1], A.mult, A.add, ["pd0", "pd1"], ["pd4"])
     ts(pd[5], a6, float(NA), pd[2], A.mult, A.add, ["pcf", "pd2"], ["pd5"])
@@ -346,11 +394,11 @@ def rank_program(g, core, T, topo):
     ts(T.pmu[:, 0:2 * NA], T.pmf[:, 0:2 * NA], pd[5], None, A.add, None, ["pmf0", "pd5"], ["pmH0"])
     ts(T.pmu[:, 2 * NA:16], T.pmf[:, 2 * NA:16], pd[6], 6.0 * NA, A.add, A.add, ["pmf0", "pd6"], ["pmH"])
     cp(T.cf[:], T.hsi[:].indirect(T.pmu[:, 36:40]), ["hsi", "pmN"], ["cf"])
-    ts(T.ident[:], T.cc[:, 0:128], pf, None, A.is_equal, None, ["cc", "pcf"], ["ident"])
-    cp(T.cu[:], T.cf[:].indirect(T.pmu[:, 32:36]), ["cf", "pm64"], ["cu"])
     cp(T.offu[:], T.homi[:].indirect(T.pmu[:, 0:16]), ["homi", "pmH0", "pmH"], ["offu"])
-    suscept()
-    halves(0)
+    for j in range(3):
+        sus_gather(j)
+    sus_turn("a", 0)
+    sus_turn("a", 1)
     ts(pd[8], a7, 8.0, None, A.mult, None, ["pcf"], ["pd8"])
     ts(pd[9], f4, 0.0, 128.0, A.is_equal, A.mult, ["pcf"], ["pd9"])
     ts(pd[10], f4, 2.0, -64.0, A.is_equal, A.mult, ["pcf"], ["pd10"])
@@ -368,7 +416,8 @@ def rank_program(g, core, T, topo):
     for k in range(4):
         ts(T.wz[:, 128 * k:128 * k + 128], T.wz0[:], col(T.m4, k), None, A.mult, None, ["wz0", "m4"], ["wq%d" % k])
     cp(T.awyf[:], T.awyi[:].indirect(T.pmu[:, 0:16]), ["awyi", "pmH0", "pmH"], ["awyf"])
-    next_code()
+    for j in range(4):
+        next_code(j)
     tt(T.dif[:], T.awyf[:], T.homf[:], A.subtract, ["awyf", "homf"], ["dif"])
 
     for d in range(D):
@@ -383,19 +432,24 @@ def rank_program(g, core, T, topo):
                                         ["g%d_%d" % (b, c) for c in range(c0, c1)])
 
         def press(b, c0=0, c1=4):
-            bank, o = (("p0", b) if b < 4 else ("p1", b - 4) if b < 6 else ("p%d" % (b - 4), 0))
+            k = max(i for i in range(len(PB)) if sum(PB[:i]) <= b)
+            bank, o = "p%d" % k, b - sum(PB[:k])
             pe([(T[bank][:, 128 * o:128 * o + 128], T.gth[:, 512 * b + 128 * c:512 * b + 128 * c + 128], T.ident[:],
                  c == 0, c == 3) for c in range(c0, c1)], ["g%d_%d" % (b, c) for c in range(c0, c1)] + ["ident"], [bank])
 
-        def score(bank, c0, n):
-            tt(T.sc[:, c0:c0 + n], T[bank][:, 0:n], T.st[:, c0:c0 + n], A.mult, [bank, "st0", "st1"], ["sc" + bank])
+        def score(k):
+            bank, c0, n = "p%d" % k, 128 * sum(PB[:k]), 128 * PB[k]
+            tt(T.sc[:, c0:c0 + n], T[bank][:, 0:n], T.st[:, c0:c0 + n], A.mult,
+               [bank, "st%d" % (c0 // 512), "st%d" % ((c0 + n - 1) // 512)], ["sc" + bank])
 
-        def best(bank, c0, n):
+        def best(k):
+            bank, c0, n = "p%d" % k, 128 * sum(PB[:k]), 128 * PB[k]
             v(lambda: V.tensor_tensor_scan(T.kk[:, c0:c0 + n], T.d0[:, 0:n], T.sc[:, c0:c0 + n], 0.0, A.add, A.max),
               ["d0", "sc" + bank], ["kk" + bank])
 
         def event(nm, step):
-            j0, j1, banks = (0, 8 * NA, ["p0", "p1"]) if nm == "A" else (8 * NA, 64, ["p2", "p3"])
+            j0, j1 = (0, 8 * NA) if nm == "A" else (8 * NA, 64)
+            banks = ["p%d" % k for k in range(len(PB)) if (sum(PB[:k]) < NA) == (nm == "A")]
             if step == 0:
                 ts(T.ki[:, j0:j1], T.kk[:, 16 * j0 + 15:16 * j1:16], float(32 * TH + 16), None, A.max, None,
                    ["kk" + b for b in banks], ["ki" + nm])
@@ -420,66 +474,41 @@ def rank_program(g, core, T, topo):
             if last:
                 load("s", T.y[:, c0:c0 + n], T.ybuf[:, c0:c0 + n], [key], ["y%d" % i])
 
-        for eng, b in (("a", 2), ("v", 0), ("a", 3), ("v", 1), ("a", 5), ("v", 4), ("a", 6)):
-            gat(eng, b)
-        gat("a", 7, 0, 3)
-        gat("a", 7, 3, 4)
-        for b in (0, 2, 1, 3, 4, 5, 6):
-            press(b)
-        press(7, 0, 3)
-        press(7, 3, 4)
-        score("p0", 0, 512)
-        best("p0", 0, 512)
-        score("p1", 512, 256)
-        best("p1", 512, 256)
-        score("p2", 768, 128)
-        event("A", 0)
-        best("p2", 768, 128)
-        event("A", 1)
-        score("p3", 896, 128)
-        event("A", 2)
-        best("p3", 896, 128)
-        event("A", 3)
-        spread("z0", 0, 2, "A")
-        spread("z1", 2, 4, "A")
+        def spreads(nm):
+            zs = [z[0] for z in ZB if (z[1] < 128 * NA) == (nm == "A")]
+            n = 4 // len(zs)
+            for i, zn in enumerate(zs):
+                spread(zn, n * i, n * i + n, nm)
+
+        def steps(order_):
+            for w in order_.split():
+                c, k = w[0], w[1:]
+                if c in "AE":
+                    event("A" if c == "A" else "B", int(k))
+                elif c == "Z":
+                    spreads("A" if k == "A" else "B")
+                elif c == "M":
+                    masks("a", k or "AB", 0, 8)
+                elif c == "X":
+                    fix()
+                elif c == "T":
+                    sus_turn(k[0], int(k[1]))
+                elif c == "L":
+                    halves(d + 1, int(k), "v")
+                else:
+                    {"S": score, "B": best, "F": fresh, "H": history, "N": next_code, "U": sus_gather, "O": contacts}[c](int(k))
+
+        done = sorted((sum(x[2] - x[1] for x in L[:i + 1]), L[i], e) for e, L in (("v", GV), ("a", GA)) for i in range(len(L)))
+        for _, x, e in done:
+            gat(e, *x)
+        for _, x, e in done:
+            press(*x)
         if last:
-            masks("a", "A", 0, 8)
-        event("B", 0)
-        event("B", 1)
-        event("B", 2)
-        event("B", 3)
-        spread("z2", 0, 4, "B")
-        if last:
-            masks("a", "B", 0, 4)
-            masks("v", "B", 4, 8)
-            fix()
-            fresh(0)
-            fresh(1)
-            fresh(2)
-            history(T.hout[:].indirect(T.pmu[:, 36:40]), "hout")
-            load("a", T.h[:], T.hout[:], ["hout"], ["h"])
-            add(pl, "s", None, ["y0", "y1", "y2", "h"], [])
-            break
-        masks("a", "AB", 0, 4)
-        fresh(0)
-        fresh(1)
-        fresh(2)
-        gather_shown(d + 1, "a", 0, 2)
-        gather_shown(d + 1, "v", 2, 4)
-        send_far(d + 1)
-        gather_shown(d + 1, "v", 4, 6)
-        gather_shown(d + 1, "a", 6, 7)
-        send_near(d + 1, [0, 1])
-        send_near(d + 1, [2])
-        masks("a", "AB", 4, 8)
-        fix()
-        halves(d + 1)
-        history(T.cf[:], "cf")
-        cp(T.cu[:], T.cf[:].indirect(T.pmu[:, 32:36]), ["cf", "pm64"], ["cu"])
-        suscept()
-        tt(T.tmpo[:], T.hit[:].indirect(T.pmu[:, 16:32]), T.dif[:], A.mult, ["hit", "pmI", "dif"], ["tmpo"])
-        tt(T.offf[:], T.tmpo[:], T.homf[:], A.add, ["tmpo", "homf"], ["offf"])
-        cp(T.offu[:], T.offf[:], ["offf"], ["offu"])
-        next_code()
+            steps(LAST)
+            add(pl, "s", None, ["y%d" % i for i in range(len(ZB))] + ["h"], [])
+        else:
+            steps(DAY)
+            exchange(d + 1)
+            steps(BETWEEN)
     emit(pl, queues, T)
     g.wait_ge(T.sem.sent, sent[0])

from concourse.bass import DstId, RemoteDMATransfer
from concourse.mybir import AluOpType, ActivationFunctionType

P, S, D, TH = 1024, 160, 3, 11008
W = P + 7 * S
NSEM = 70
BF, F32, I32, U16 = "bfloat16", "float32", "int32", "uint16"
SCRATCH = {}
for _d in range(D):
    SCRATCH["win%d" % _d] = ("sbuf", [128, W], BF)
    SCRATCH["snd%d" % _d] = ("sbuf", [128, 7 * S], BF)
for _n, _c, _t in (
        ("ybuf", P, F32), ("susb", 2048, BF), ("shi", 70, I32), ("shu", 70, U16), ("homi", 256, I32), ("awyi", 256, I32),
        ("homf", 256, F32), ("awyf", 256, F32), ("dif", 256, F32), ("tmpo", 256, F32), ("offf", 256, F32), ("offu", 256, U16),
        ("hsi", 64, I32), ("cf", 64, F32), ("cu", 64, U16), ("ci", 64, I32), ("c7", 64, I32), ("ct", 64, F32), ("af", 64, F32),
        ("hit", 64, F32), ("uu", 64, F32), ("tt", 64, F32), ("hout", 64, F32),
        ("gth", 4096, BF), ("sg", P, BF), ("st", P, BF), ("sc", P, F32), ("kk", P, F32), ("ki", 64, I32), ("ri", 64, I32),
        ("ee", 256, BF), ("et", 256, BF), ("rr", 512, BF), ("hy", P, BF), ("half", P, BF),
        ("ident", 128, BF), ("d0", 256, BF), ("wz0", 128, BF), ("wz", 512, BF), ("m4", 4, F32), ("mk", 8, F32),
        ("wd", 240, BF), ("pci", 10, I32), ("pcf", 10, F32), ("pd", 16, F32), ("cc", 240, F32), ("pmf", 32, F32), ("pmu", 40, U16),
        ("ia", 128, F32), ("ib", 128, F32), ("wa", 128, F32), ("wb", 128, F32), ("wc", 128, F32), ("we", 128, F32)):
    SCRATCH[_n] = ("sbuf", [128, _c], _t)
NA = 6
PB = (2, 2, 2, 1, 1)
ZB = (("z0", 0, 384), ("z1", 384, 384), ("z2", 768, 256))
GV = ((0, 0, 4), (2, 0, 4), (4, 0, 4))
GA = ((1, 0, 4), (3, 0, 4), (5, 0, 4), (6, 0, 4), (7, 0, 3), (7, 3, 4))
FAR_CALLS = ((0, 1), (2, 3))
DAY = "S0 S1 B0 S2 B1 B2 S3 A0 B3 A1 S4 A2 B4 A3 ZA E0 E1 E2 M F0 E3 ZE X F1 F2"
LAST = "S0 S1 B0 S2 B1 B2 S3 A0 B3 A1 S4 A2 B4 A3 ZA MA E0 E1 E2 MB F0 E3 ZE X F1 F2 H0 H1 H3"
BETWEEN = "H0 H1 H2 U0 U1 U2 Ta0 Ta1 O0 N0 L0 N1 O1 N2 O2 N3 L1"
for _n in ["p%d" % _i for _i in range(len(PB))] + [_z[0] for _z in ZB]:
    SCRATCH[_n] = ("psum", [128, 512], F32)
SEMAPHORES = ["sent", "arr0", "arr1", "arr2", "rin0", "rin1", "rin2"] + ["s%d" % _i for _i in range(NSEM)]

A = AluOpType
ACT = ActivationFunctionType


def routes(T, topo):
    cores = list(T.cores)
    out = []
    for r, c in enumerate(cores):
        near = [q for q, x in enumerate(cores) if q != r and topo.may_write(c, x)]
        far = [q for q, x in enumerate(cores) if q != r and not topo.may_write(c, x)]
        hs = [x for x in topo.cores_of(c) if x not in cores and all(topo.may_write(x, cores[q]) for q in far)]
        same = [x for x in hs if topo.die(x) == topo.die(c)]
        other = [x for x in hs if topo.die(x) != topo.die(c)]
        hs = [x for pair in zip(same, other) for x in pair]
        ring = sorted(near + [r])
        i = ring.index(r)
        n = len(hs)
        by_helper = [None] * n
        for j, q in enumerate(far):
            by_helper[(i + j) % n] = q
        near = [ring[(i + t) % len(ring)] for t in range(1, len(ring))]
        out.append(([(by_helper[t], hs[t]) for t in range(n)], near))
    return out


def bits(es):
    m = 0
    for e in es:
        m |= 1 << e
    return m


def near_masks(c, cores, near, topo):
    e = topo.engines(c, cores[near[0]])
    h = len(e) // 2
    return [e[:h], e[h:], e]


def slot(r, q):
    return P + S * (r if r < q else r - 1)


def add(pl, q, fn, reads=(), writes=(), dma=False, acc=False, ext=None):
    i = len(pl["ops"])
    deps = set()
    for k in reads:
        st = pl["keys"].setdefault(k, [[], []])
        deps.update(st[0])
    for k in writes:
        st = pl["keys"].setdefault(k, [[], []])
        deps.update(st[1])
        deps.update(w for w in st[0] if not (acc and pl["ops"][w]["q"] == q))
    for k in reads:
        pl["keys"][k][1].append(i)
    for k in writes:
        st = pl["keys"][k]
        if acc and not st[1]:
            st[0].append(i)
        else:
            pl["keys"][k] = [[i], []]
    deps.discard(i)
    pl["ops"].append({"q": q, "fn": fn, "deps": deps, "dma": dma, "ext": ext})


def emit(pl, queues, T):
    ops = pl["ops"]
    know = {q: set() for q in queues}
    for i, o in enumerate(ops):
        if o["ext"]:
            o["know"], o["waits"], o["before"] = {i}, [], set()
            continue
        kn = know[o["q"]]
        o["waits"] = []
        for j in sorted(o["deps"], reverse=True):
            if j not in kn:
                o["waits"].append(j)
                kn |= ops[j]["know"]
                ops[j]["need"] = True
        o["before"] = set(kn)
        o["know"] = set(kn) | {i}
    sems = []
    for i, o in enumerate(ops):
        if o["ext"]:
            o["tok"] = o["ext"]
            continue
        eng = queues[o["q"]]
        for j in o["waits"]:
            eng.wait_ge(T.sem[ops[j]["tok"][0]], ops[j]["tok"][1])
        if o["fn"] is None:
            continue
        ins = o["fn"]()
        if o.get("need"):
            n = 16 if o["dma"] else 1
            pick = None
            for s in sems:
                if s[2] == o["dma"] and s[1] in o["before"]:
                    pick = s
                    break
            if pick is None:
                pick = ["s%d" % len(sems), i, o["dma"], 0]
                sems.append(pick)
            pick[1] = i
            pick[3] += n
            o["tok"] = (pick[0], pick[3])
            ins.then_inc(T.sem[pick[0]], n)


def helper_program(g, core, T, topo, r, q):
    cores = list(T.cores)
    rid, pid = topo.addr(cores[q], core)
    n_in = len(topo.engines(cores[r], core)) // len(FAR_CALLS[0])
    e = topo.engines(core, cores[q])
    for d in range(D):
        g.wait_ge(T.sem["rin%d" % d], n_in)
        c0 = slot(r, q)
        g.remote_dma(T["win%d" % d][:, c0:c0 + S], T["snd%d" % d][:, 0:S], T.sem["arr%d" % d], T.sem.sent, pid, rid, bits(e))
    g.wait_ge(T.sem.sent, D * len(e))


def rank_program(g, core, T, topo):
    rt = routes(T, topo)
    cores = list(T.cores)
    rank = T.rank_of(core)
    if rank is None:
        for r in range(len(cores)):
            for q, h in rt[r][0]:
                if h == core:
                    helper_program(g, core, T, topo, r, q)
        return
    far, near = rt[rank]
    n_arr = 0
    for r in range(len(cores)):
        for q, h in rt[r][0]:
            if q == rank:
                n_arr += len(topo.engines(h, core))
        if rank in rt[r][1]:
            n_arr += len(near_masks(cores[r], cores, rt[r][1], topo)[rt[r][1].index(rank)])
    order = [q for q, h in far] + near
    V, AC, PE, SY = g.vector, g.scalar, g.tensor, g.sync
    queues = {"v": V, "a": AC, "p": PE, "s": SY, "g": g}
    pl = {"ops": [], "keys": {}}
    sent = [0]

    def v(fn, r, w):
        add(pl, "v", fn, r, w)

    def a(fn, r, w):
        add(pl, "a", fn, r, w)

    def pe(mms, r, w):
        def fn():
            ins = None
            for m in mms:
                ins = PE.matmul(*m)
            return ins
        add(pl, "p", fn, r, w, acc=True)

    def load(qn, out, in_, r, w):
        add(pl, qn, lambda: queues[qn].dma_start(out, in_), r, w, dma=True)

    def ts(out, in0, s1, s2, op0, op1, r, w):
        if op1 is None:
            v(lambda: V.tensor_scalar(out, in0, s1, None, op0), r, w)
        else:
            v(lambda: V.tensor_scalar(out, in0, s1, s2, op0, op1), r, w)

    def tt(out, in0, in1, op, r, w):
        v(lambda: V.tensor_tensor(out, in0, in1, op), r, w)

    def cp(out, in_, r, w):
        v(lambda: V.tensor_copy(out, in_), r, w)

    def acp(out, in_, r, w, scale=1.0):
        a(lambda: AC.activation(out, in_, ACT.Copy, scale=scale), r, w)

    def iota(out, pat, base, cm, w, flt=True):
        if flt:
            add(pl, "g", lambda: g.iota(out, pat, base, cm, allow_small_or_imprecise_dtypes=True), [], w)
        else:
            add(pl, "g", lambda: g.iota(out, pat, base, cm), [], w)

    def own(d):
        return ["o%d_%d" % (i, d) for i in range(len(ZB))]

    def conv_shown(t0, t1):
        for t in range(t0, t1):
            q = order[t]
            k = q if q < rank else q - 1
            cp(T.shu[:, 10 * t:10 * t + 10], T.shi[:, 10 * k:10 * k + 10], ["shi"], ["shu%d" % t])

    def gather_shown(d, eng, t0, t1):
        src = T["win%d" % d][:, 0:P].indirect(T.shu[:, 10 * t0:10 * t1])
        (acp if eng == "a" else cp)(T["snd%d" % d][:, S * t0:S * t1], src, own(d) + ["shu%d" % t for t in range(t0, t1)],
                                    ["snd%d_%d" % (d, t) for t in range(t0, t1)])

    def send_far(d, ts_):
        def fn():
            trs = []
            for i, t in enumerate(ts_):
                q, h = far[t]
                rid, pid = topo.addr(h, core)
                e = topo.engines(core, h)[i::len(ts_)]
                trs.append(RemoteDMATransfer(dst_ids=[DstId(rid=rid, pnc=pid)], dma_engine_mask=bits(e),
                                             remote_sem=T.sem["rin%d" % d], src=T["snd%d" % d][:, S * t:S * t + S],
                                             dst=T["snd%d" % d][:, 0:S]))
                sent[0] += len(e)
            return g.remote_dma_fused(trs, local_sem=T.sem.sent)
        add(pl, "g", fn, ["snd%d_%d" % (d, t) for t in ts_], [])

    def exchange(d):
        for ts_ in FAR_CALLS:
            h = len(ts_) // 2
            gather_shown(d, "a", ts_[0], ts_[0] + h)
            gather_shown(d, "v", ts_[h], ts_[h] + h)
            send_far(d, ts_)
        gather_shown(d, "a", 4, 6)
        if d == 0:
            gather_shown(d, "v", 6, 7)
        else:
            gather_shown(d, "a", 6, 7)
        send_near(d, [0, 1])
        send_near(d, [2])

    def send_near(d, js):
        def fn():
            trs = []
            for j in js:
                q = near[j]
                rid, pid = topo.addr(cores[q], core)
                e = near_masks(core, cores, near, topo)[j]
                c0 = slot(rank, q)
                trs.append(RemoteDMATransfer(dst_ids=[DstId(rid=rid, pnc=pid)], dma_engine_mask=bits(e),
                                             remote_sem=T.sem["arr%d" % d], src=T["snd%d" % d][:, S * (4 + j):S * (5 + j)],
                                             dst=T["win%d" % d][:, c0:c0 + S]))
                sent[0] += len(e)
            return g.remote_dma_fused(trs, local_sem=T.sem.sent)
        add(pl, "g", fn, ["snd%d_%d" % (d, 4 + j) for j in js], [])

    def col(t, j):
        return t[:, j:j + 1]

    def masks(eng, nm, u0, u1):
        j0, j1 = {"A": (0, 8 * NA), "B": (8 * NA, 64), "AB": (0, 64)}[nm]
        for u in range(u0, u1):
            out, in_ = T.rr[:, 64 * u + j0:64 * u + j1], T.ee[:, 4 * j0:4 * j1:4]
            r, w = ["e" + x for x in nm] + ["mk"], ["rr%s%d" % (x, u) for x in nm]
            if eng == "a":
                a(lambda out=out, in_=in_, u=u: AC.activation(out, in_, ACT.Identity, scale=col(T.mk, u)), r, w)
            else:
                ts(out, in_, col(T.mk, u), None, A.mult, None, r, w)

    def fix():
        pe([(T.p0[:, 0:64], T.wd[:, 112 - 16 * k:240 - 16 * k], T.rr[:, k:512:8], k == 0, k == 7) for k in range(8)],
           ["wd"] + ["rr%s%d" % (nm, u) for nm in "AB" for u in range(8)], ["p0"])

    def history(j):
        if j == 0:
            ts(T.hit[:], T.p0[:, 0:64], 16.0, None, A.is_lt, None, ["p0"], ["hit"])
            tt(T.uu[:], T.af[:], T.p0[:, 0:64], A.subtract, ["af", "p0"], ["uu"])
        elif j == 1:
            tt(T.tt[:], T.uu[:], T.hit[:], A.mult, ["uu", "hit"], ["tt"])
        elif j == 2:
            tt(T.cf[:], T.tt[:], T.cf[:], A.add, ["tt", "cf"], ["cf"])
        else:
            tt(T.hout[:].indirect(T.pmu[:, 36:40]), T.tt[:], T.cf[:], A.add, ["tt", "cf", "pmN"], ["hout"])
            load("a", T.h[:], T.hout[:], ["hout"], ["h"])

    def sus_gather(j):
        if j == 0:
            cp(T.cu[:], T.cf[:].indirect(T.pmu[:, 32:36]), ["cf", "pm64"], ["cu"])
        else:
            k = j - 1
            acp(T.sg[:, 512 * k:512 * k + 512], T.susb[:, 0:2048].indirect(T.cu[:, 32 * k:32 * k + 32]), ["susb", "cu"],
                ["sg%d" % k], scale=32.0)

    def sus_turn(eng, k):
        bank = "p%d" % (k + 1)
        for b in range(4):
            pe([(T[bank][:, 128 * b:128 * b + 128], T.sg[:, 512 * k + 128 * b:512 * k + 128 * b + 128], T.ident[:], True, True)],
               ["sg%d" % k, "ident"], [bank])
        (acp if eng == "a" else cp)(T.st[:, 512 * k:512 * k + 512], T[bank][:], [bank], ["st%d" % k])

    def halves(d, j, eng):
        if j == 0:
            if eng == "a":
                a(lambda: AC.activation(T.hy[:], T["win%d" % d][:, 0:P], ACT.Copy, scale=0.5, bias=127.8), own(d), ["hy"])
            else:
                ts(T.hy[:], T["win%d" % d][:, 0:P], 0.5, 127.8, A.mult, A.add, own(d), ["hy"])
            return
        if eng == "a":
            a(lambda: AC.activation(T.half[:], T.hy[:], ACT.Copy, bias=-128.0), ["hy"], ["half"])
        else:
            ts(T.half[:], T.hy[:], 128.0, None, A.subtract, None, ["hy"], ["half"])
        for zn, c0, n in ZB:
            pe([(T[zn][:, 0:n], T.ident[:], T.half[:, c0:c0 + n], True, False)], ["ident", "half"], [zn])

    def next_code(j):
        if j == 0:
            cp(T.ci[:], T.cf[:], ["cf"], ["ci"])
        elif j == 1:
            ts(T.c7[:], T.ci[:], 127, None, A.bitwise_and, None, ["ci"], ["c7"])
        elif j == 2:
            ts(T.ct[:], T.c7[:], 16.0, 15.0, A.mult, A.add, ["c7"], ["ct"])
        else:
            tt(T.af[:], T.ct[:], T.cf[:], A.subtract, ["ct", "cf"], ["af"])

    def contacts(j):
        if j == 0:
            tt(T.tmpo[:], T.hit[:].indirect(T.pmu[:, 16:32]), T.dif[:], A.mult, ["hit", "pmI", "dif"], ["tmpo"])
        elif j == 1:
            tt(T.offf[:], T.tmpo[:], T.homf[:], A.add, ["tmpo", "homf"], ["offf"])
        else:
            cp(T.offu[:], T.offf[:], ["offf"], ["offu"])

    load("s", T.win0[:, 0:P], T.x[:], [], own(0))
    load("a", T.shi[:], T.shown[:], [], ["shi"])
    load("s", T.susb[:], T.sus[:], [], ["susb"])
    load("s", T.hsi[:], T.hist[:], [], ["hsi"])
    load("s", T.homi[:], T.home[:], [], ["homi"])
    load("s", T.awyi[:], T.away[:], [], ["awyi"])
    iota(col(T.pci, 6), [[0, 1]], 0, 1, ["pi"], flt=False)
    iota(T.pmf[:, 0:16], [[2, 8], [128, 2]], 0, 0, ["pmf0"])
    iota(T.pmf[:, 16:32], [[1, 8], [0, 2]], 0, 0, ["pmf1"])
    iota(T.cc[:], [[1, 240]], 0, 0, ["cc"])
    iota(T.ia[:], [[1, 8], [0, 16]], 0, 0, ["ia"])
    iota(T.ib[:], [[0, 8], [-1, 16]], 15, 0, ["ib"])
    v(lambda: V.memset(T.d0[:], 1.0), [], ["d0"])
    v(lambda: V.memset(T.ee[:], 1.0), [], ["eA", "qA", "eB", "qB"])
    v(lambda: V.memset(T.hout[:], 0.0), [], ["hout"])
    v(lambda: V.memset(T.d0[:, 0:256:16], -3.0e7), [], ["d0"])
    pi = col(T.pci, 6)
    ts(col(T.pci, 0), pi, 7, None, A.bitwise_and, None, ["pi"], ["pc0"])
    ts(col(T.pci, 1), pi, 3, 1, A.arith_shift_right, A.bitwise_and, ["pi"], ["pc1"])
    ts(col(T.pci, 2), pi, 15, None, A.bitwise_and, None, ["pi"], ["pc2"])
    ts(col(T.pci, 3), pi, 4, None, A.arith_shift_right, None, ["pi"], ["pc3"])
    ts(col(T.pci, 4), pi, 3, None, A.bitwise_and, None, ["pi"], ["pc4"])
    ts(col(T.pci, 5), pi, 31, 2, A.bitwise_and, A.arith_shift_right, ["pi"], ["pc5"])
    ts(col(T.pci, 7), pi, 5, None, A.arith_shift_right, None, ["pi"], ["pc6"])
    ts(col(T.pci, 8), pi, 1, None, A.bitwise_and, None, ["pi"], ["pc7"])
    ts(col(T.pci, 9), pi, 6, None, A.bitwise_and, None, ["pi"], ["pc8"])
    cp(T.pcf[:], T.pci[:], ["pi"] + ["pc%d" % j for j in range(9)], ["pcf"])
    a7, hh, q16, uc, f4, g8, pf, quad, b1, a6 = [col(T.pcf, j) for j in range(10)]
    pd = [col(T.pd, j) for j in range(16)]
    ts(T.ident[:], T.cc[:, 0:128], pf, None, A.is_equal, None, ["cc", "pcf"], ["ident"])
    ts(pd[0], a7, float(NA), None, A.is_ge, None, ["pcf"], ["pd0"])
    ts(pd[1], a7, 2.0, hh, A.mult, A.add, ["pcf"], ["pd1"])
    ts(pd[2], hh, 64.0, b1, A.mult, A.add, ["pcf"], ["pd2"])
    ts(pd[7], a7, 8.0, hh, A.mult, A.add, ["pcf"], ["pd7"])
    conv_shown(0, 7)
    exchange(0)
    halves(0, 0, "a")
    halves(0, 1, "a")
    ts(pd[3], pd[0], 16.0 - 4 * NA, 2.0 * NA, A.mult, A.add, ["pd0"], ["pd3"])
    ts(pd[4], pd[0], 6.0 * NA, pd[1], A.mult, A.add, ["pd0", "pd1"], ["pd4"])
    ts(pd[5], a6, float(NA), pd[2], A.mult, A.add, ["pcf", "pd2"], ["pd5"])
    ts(pd[6], a6, 8.0 - NA, pd[2], A.mult, A.add, ["pcf", "pd2"], ["pd6"])
    ts(T.pmu[:, 32:36], T.cc[:, 0:8:2], pd[7], None, A.add, None, ["cc", "pd7"], ["pm64"])
    ts(T.pmu[:, 36:40], T.cc[:, 0:4], pd[3], pd[4], A.mult, A.add, ["cc", "pd3", "pd4"], ["pmN"])
    ts(T.pmu[:, 0:2 * NA], T.pmf[:, 0:2 * NA], pd[5], None, A.add, None, ["pmf0", "pd5"], ["pmH0"])
    ts(T.pmu[:, 2 * NA:16], T.pmf[:, 2 * NA:16], pd[6], 6.0 * NA, A.add, A.add, ["pmf0", "pd6"], ["pmH"])
    cp(T.cf[:], T.hsi[:].indirect(T.pmu[:, 36:40]), ["hsi", "pmN"], ["cf"])
    cp(T.offu[:], T.homi[:].indirect(T.pmu[:, 0:16]), ["homi", "pmH0", "pmH"], ["offu"])
    for j in range(3):
        sus_gather(j)
    sus_turn("a", 0)
    sus_turn("a", 1)
    ts(pd[8], a7, 8.0, None, A.mult, None, ["pcf"], ["pd8"])
    ts(pd[9], f4, 0.0, 128.0, A.is_equal, A.mult, ["pcf"], ["pd9"])
    ts(pd[10], f4, 2.0, -64.0, A.is_equal, A.mult, ["pcf"], ["pd10"])
    ts(pd[11], f4, 1.0, -64.0, A.is_equal, A.mult, ["pcf"], ["pd11"])
    ts(T.pmu[:, 16:32], T.pmf[:, 16:32], pd[8], None, A.add, None, ["pmf1", "pd8"], ["pmI"])
    ts(T.wb[:], T.ib[:], pd[10], pd[9], A.mult, A.add, ["ib", "pd9", "pd10"], ["wb"])
    ts(T.wa[:], T.ia[:], g8, None, A.is_equal, None, ["ia", "pcf"], ["wa"])
    ts(T.mk[:], T.cc[:, 0:8], uc, None, A.is_equal, None, ["cc", "pcf"], ["mk"])
    tt(T.wc[:], T.wb[:], T.ib[:], A.mult, ["wb", "ib"], ["wc"])
    ts(T.m4[:], T.cc[:, 0:4], quad, None, A.is_equal, None, ["cc", "pcf"], ["m4"])
    ts(T.we[:], T.wc[:], pd[11], pd[10], A.add, A.subtract, ["wc", "pd10", "pd11"], ["we"])
    ts(T.wd[:], T.cc[:], 112.0, q16, A.subtract, A.is_equal, ["cc", "pcf"], ["wd"])
    tt(T.wz0[:], T.wa[:], T.we[:], A.mult, ["wa", "we"], ["wz0"])
    cp(T.homf[:], T.homi[:].indirect(T.pmu[:, 0:16]), ["homi", "pmH0", "pmH"], ["homf"])
    for k in range(4):
        ts(T.wz[:, 128 * k:128 * k + 128], T.wz0[:], col(T.m4, k), None, A.mult, None, ["wz0", "m4"], ["wq%d" % k])
    cp(T.awyf[:], T.awyi[:].indirect(T.pmu[:, 0:16]), ["awyi", "pmH0", "pmH"], ["awyf"])
    for j in range(4):
        next_code(j)
    tt(T.dif[:], T.awyf[:], T.homf[:], A.subtract, ["awyf", "homf"], ["dif"])

    for d in range(D):
        last = d == D - 1
        win = T["win%d" % d]
        add(pl, "x", None, [], ["slots%d" % d], ext=("arr%d" % d, n_arr))
        wk = own(d) + ["slots%d" % d, "offu"]

        def gat(eng, b, c0=0, c1=4):
            (acp if eng == "a" else cp)(T.gth[:, 512 * b + 128 * c0:512 * b + 128 * c1],
                                        win[:, 0:W].indirect(T.offu[:, 32 * b + 8 * c0:32 * b + 8 * c1]), wk,
                                        ["g%d_%d" % (b, c) for c in range(c0, c1)])

        def press(b, c0=0, c1=4):
            k = max(i for i in range(len(PB)) if sum(PB[:i]) <= b)
            bank, o = "p%d" % k, b - sum(PB[:k])
            pe([(T[bank][:, 128 * o:128 * o + 128], T.gth[:, 512 * b + 128 * c:512 * b + 128 * c + 128], T.ident[:],
                 c == 0, c == 3) for c in range(c0, c1)], ["g%d_%d" % (b, c) for c in range(c0, c1)] + ["ident"], [bank])

        def score(k):
            bank, c0, n = "p%d" % k, 128 * sum(PB[:k]), 128 * PB[k]
            tt(T.sc[:, c0:c0 + n], T[bank][:, 0:n], T.st[:, c0:c0 + n], A.mult,
               [bank, "st%d" % (c0 // 512), "st%d" % ((c0 + n - 1) // 512)], ["sc" + bank])

        def best(k):
            bank, c0, n = "p%d" % k, 128 * sum(PB[:k]), 128 * PB[k]
            v(lambda: V.tensor_tensor_scan(T.kk[:, c0:c0 + n], T.d0[:, 0:n], T.sc[:, c0:c0 + n], 0.0, A.add, A.max),
              ["d0", "sc" + bank], ["kk" + bank])

        def event(nm, step):
            j0, j1 = (0, 8 * NA) if nm == "A" else (8 * NA, 64)
            banks = ["p%d" % k for k in range(len(PB)) if (sum(PB[:k]) < NA) == (nm == "A")]
            if step == 0:
                ts(T.ki[:, j0:j1], T.kk[:, 16 * j0 + 15:16 * j1:16], float(32 * TH + 16), None, A.max, None,
                   ["kk" + b for b in banks], ["ki" + nm])
            elif step == 1:
                ts(T.ri[:, j0:j1], T.ki[:, j0:j1], 31, None, A.bitwise_and, None, ["ki" + nm], ["ri" + nm])
            elif step == 2:
                cp(T.ee[:, 4 * j0:4 * j1:4], T.ri[:, j0:j1], ["ri" + nm], ["e" + nm])
                tt(T.ee[:, 4 * j0 + 1:4 * j1:4], T.ri[:, j0:j1], T.ri[:, j0:j1], A.mult, ["ri" + nm], ["q" + nm])
            else:
                v(lambda: V.transpose(T.et[:, 4 * j0:4 * j1], T.ee[:, 4 * j0:4 * j1]), ["e" + nm, "q" + nm], ["et" + nm])

        def spread(zn, k0, k1, nm):
            c0, n = (0, 32 * NA) if nm == "A" else (32 * NA, 256 - 32 * NA)
            pe([(T[zn][:, n * (k - k0):n * (k - k0) + n], T.wz[:, 128 * k:128 * k + 128], T.et[:, c0:c0 + n], False, k == k1 - 1)
                for k in range(k0, k1)], ["wq0", "wq1", "wq2", "wq3", "et" + nm], [zn])

        def fresh(i):
            zn, c0, n = ZB[i]
            key = own(d + 1)[i]
            out = T.ybuf if last else T["win%d" % (d + 1)]
            tt(out[:, c0:c0 + n], T[zn][:, 0:n], T.half[:, c0:c0 + n], A.max, [zn, "half"], [key])
            if last:
                load("s", T.y[:, c0:c0 + n], T.ybuf[:, c0:c0 + n], [key], ["y%d" % i])

        def spreads(nm):
            zs = [z[0] for z in ZB if (z[1] < 128 * NA) == (nm == "A")]
            n = 4 // len(zs)
            for i, zn in enumerate(zs):
                spread(zn, n * i, n * i + n, nm)

        def steps(order_):
            for w in order_.split():
                c, k = w[0], w[1:]
                if c in "AE":
                    event("A" if c == "A" else "B", int(k))
                elif c == "Z":
                    spreads("A" if k == "A" else "B")
                elif c == "M":
                    masks("a", k or "AB", 0, 8)
                elif c == "X":
                    fix()
                elif c == "T":
                    sus_turn(k[0], int(k[1]))
                elif c == "L":
                    halves(d + 1, int(k), "v")
                else:
                    {"S": score, "B": best, "F": fresh, "H": history, "N": next_code, "U": sus_gather, "O": contacts}[c](int(k))

        done = sorted((sum(x[2] - x[1] for x in L[:i + 1]), L[i], e) for e, L in (("v", GV), ("a", GA)) for i in range(len(L)))
        for _, x, e in done:
            gat(e, *x)
        for _, x, e in done:
            press(*x)
        if last:
            steps(LAST)
            add(pl, "s", None, ["y%d" % i for i in range(len(ZB))] + ["h"], [])
        else:
            steps(DAY)
            exchange(d + 1)
            steps(BETWEEN)
    emit(pl, queues, T)
    g.wait_ge(T.sem.sent, sent[0])
